import numpy as np
import ml_dtypes


def mxq(x, axis, fmt="e4m3"):
    dtype, down = {"e4m3": (ml_dtypes.float8_e4m3fn, 7), "e5m2": (ml_dtypes.float8_e5m2, 14)}[fmt]
    v = np.moveaxis(np.asarray(x, np.float32).astype(ml_dtypes.bfloat16).astype(np.float64), axis, -1)
    blocks = v.reshape(v.shape[:-1] + (-1, 32))
    amax = np.abs(blocks).max(-1, keepdims=True)
    byte = np.maximum(np.where(amax > 0, np.frexp(amax)[1] - 1 + 127, 0) - down, 1)
    scale = np.exp2(byte - 127.0)
    codes = (blocks / scale).astype(np.float32).astype(dtype).astype(np.float64)
    return np.moveaxis((codes * scale).reshape(v.shape), -1, axis)


WIDE = False


def mx_kscale(k):
    if not WIDE:
        return np.ones(k)
    levels = np.array([10, -10, 5, -5, 0])
    if k % 512:
        return np.exp2(np.random.permutation(np.resize(levels, k // 32))).repeat(32)
    a = np.empty((k // 512, 16))
    for p in range(k // 512):
        a[p, :8] = np.random.permutation(np.resize(levels, 8))
        for g in range(8):
            far = levels[np.abs(levels - a[p, g]) >= 10]
            a[p, g + 8] = far[np.random.randint(len(far))]
    return np.exp2(a.ravel()).repeat(32)


BF16 = ml_dtypes.bfloat16


def bf(x):
    return np.asarray(x, np.float32).astype(BF16)


def f64(x):
    return np.asarray(x).astype(np.float64)

def planes(Y):
    n, m = Y.shape
    b = f64(bf(Y)).reshape(n // 32, 32, m)
    amax = np.abs(b).max(1)
    byte = np.clip(np.where(amax > 0, np.frexp(amax)[1] - 1 + 127 - 7, 1), 1, 254)
    codes = (b * np.exp2(127.0 - byte)[:, None, :]).reshape(n, m).astype(np.float32).astype(ml_dtypes.float8_e4m3fn).view(np.uint8)
    words = codes.reshape(n // 512, 128, 4, m).transpose(0, 1, 3, 2)
    return np.ascontiguousarray(words), np.ascontiguousarray(byte.astype(np.uint8).reshape(n // 512, 16, m))


Q, C, H, W, M = 2, 8, 512, 512, 512


def gelu_tanh(t):
    return 0.5 * t * (1.0 + np.tanh(np.sqrt(2.0 / np.pi) * (t + 0.044715 * (t * t * t))))


def setup_inputs():
    s = np.stack([mx_kscale(W), mx_kscale(H)])
    t = np.stack([mx_kscale(M), mx_kscale(M)])
    return {
        "x": bf(np.random.standard_normal((C, H, W))),
        "a": bf((1.0 + 0.1 * np.random.standard_normal((Q, W))) * s),
        "f": bf(np.random.standard_normal((Q, W, M)) / np.sqrt(W) / s[:, :, None]),
        "r": bf(np.random.uniform(0.5, 1.5, (Q, C, M)) * t[:, None, :]),
        "g": bf(np.random.standard_normal((Q, M, W)) / np.sqrt(M) / t[:, :, None]),
    }


def spectral_along_width(x, a0, f0, r0, g0):
    xw = x * a0[None, None, :]
    uw = mxq(xw, 2, "e4m3") @ mxq(f0, 0, "e4m3")
    vw = uw * r0[:, None, :]
    return mxq(vw, 2, "e4m3") @ mxq(g0, 0, "e4m3")


def spectral_along_height(x, a1, f1, r1, g1):
    xh = x * a1[None, :, None]
    uh = mxq(f1, 0, "e4m3").T @ mxq(xh, 1, "e4m3")
    vh = uh * r1[:, :, None]
    return mxq(g1, 0, "e4m3").T @ mxq(vh, 1, "e4m3")


def core(x, a, f, r, g):
    x, a, f, r, g = f64(x), f64(a), f64(f), f64(r), f64(g)
    yw = spectral_along_width(x, a[0], f[0], r[0], g[0])
    yh = spectral_along_height(x, a[1], f[1], r[1], g[1])
    t = yw + yh
    return gelu_tanh(t)


def reference(x, a, f, r, g):
    R_out = core(x, a, f, r, g)
    words, scales = planes(np.moveaxis(R_out, 2, 0).reshape(512, -1))
    return R_out, words, scales

@@ -1,0 +1,288 @@
+from contextlib import ExitStack
+
+import concourse.mybir as mybir
+from concourse.masks import make_identity
+
+F32 = mybir.dt.float32
+BF16 = mybir.dt.bfloat16
+I32 = mybir.dt.int32
+U32 = mybir.dt.uint32
+U8 = mybir.dt.uint8
+FP8X4 = mybir.dt.float8_e4m3fn_x4
+MULT = mybir.AluOpType.mult
+GELU = mybir.ActivationFunctionType.Gelu_apprx_tanh
+COPY = mybir.ActivationFunctionType.Copy
+
+C, S = 8, 512
+P = 128
+PACK = 4
+FLOPS = 4 * 2 * C * S * S * S
+
+ACT_BLOCKS = (0, 1, 1, 1, 1, 1, 1, 2)
+
+
+def tile_factorizedtwoaxisspectraloperator_x1_kernel(tc, x, a, f, r, g, out_0, out_1, out_2):
+    nc = tc.nc
+    words_out = out_1[0].rearrange("p m t -> p (m t)").bitcast(I32)
+    scales_out = out_2[0].bitcast(I32)
+
+    with ExitStack() as ctx:
+        keep = ctx.enter_context(tc.tile_pool(name="keep", bufs=1))
+        work = ctx.enter_context(tc.tile_pool(name="work", bufs=2))
+        psum = ctx.enter_context(tc.psum_pool(name="psum", bufs=2))
+        ctx.enter_context(tc.manual_schedule())
+
+        ident = keep.tile([P, P], F32, name="ident", align_bytes=64)
+        make_identity(nc, ident[:])
+        warm = keep.tile([P, 2], F32, name="warm")
+        nc.vector.memset(warm[:, 0:1], 0.0)
+        warm_out = keep.tile([P, 1], F32, name="warm_out")
+        nc.scalar.activation(out=warm_out[:], in_=warm[:, 0:1], func=GELU)
+
+        a_sb = keep.tile([P, 2, PACK], BF16, name="a_sb", align_bytes=64)
+        r_sb = keep.tile([P, 2 * C, PACK], BF16, name="r_sb", align_bytes=64)
+        r_f32 = keep.tile([P, 2 * C, PACK], F32, name="r_f32", align_bytes=64)
+        x_sb = [keep.tile([P, PACK, S], BF16, name="x_sb%d" % c, align_bytes=64) for c in range(C)]
+        w_names = ("f0", "f1", "g0", "g1")
+        w_hbm = {"f0": f[0], "f1": f[1], "g0": g[0], "g1": g[1]}
+        w_raw = {n: keep.tile([P, PACK, S], BF16, name="raw_" + n, align_bytes=64) for n in w_names}
+        pl_scales = keep.tile([P, C * S], U8, name="pl_scales", align_bytes=64)
+
+        def load_rows(dst, src):
+            nc.sync.dma_start(out=dst[:], in_=src.rearrange("(p j) n -> p j n", j=PACK))
+
+        nc.sync.dma_start(out=a_sb[:], in_=a.rearrange("q (p t) -> p q t", t=PACK))
+        load_rows(x_sb[0], x[0])
+        load_rows(w_raw["f0"], w_hbm["f0"])
+        load_rows(w_raw["f1"], w_hbm["f1"])
+        load_rows(x_sb[1], x[1])
+        nc.sync.dma_start(out=r_sb[:], in_=r.rearrange("q c (p t) -> p (q c) t", t=PACK))
+        load_rows(w_raw["g0"], w_hbm["g0"])
+        load_rows(x_sb[2], x[2])
+        load_rows(w_raw["g1"], w_hbm["g1"])
+        for c in range(3, C):
+            load_rows(x_sb[c], x[c])
+        nc.gpsimd.tensor_copy(out=r_f32[:], in_=r_sb[:])
+
+        grouped = {}
+        codes = {}
+        scales = {}
+        banks = {}
+        scaled = {}
+        y_sb = {}
+        y_bf = {}
+
+        def new_grouped(kind, c):
+            grouped[kind, c] = work.tile([P, S, PACK], BF16, name="grp_" + kind, align_bytes=64)
+            return grouped[kind, c]
+
+        def copy_on(engine, out, in_):
+            if engine == "act":
+                nc.scalar.copy(out=out, in_=in_)
+            else:
+                nc.vector.tensor_copy(out=out, in_=in_)
+
+        def interleave(engine, dst, src):
+            copy_on(engine, dst.rearrange("p (c i) t -> p c t i", i=4), src.rearrange("p t (c i) -> p c t i", i=4))
+
+        def group_weight(name, engine):
+            dst = work.tile([P, S, PACK], BF16, name="grp_weight", align_bytes=64)
+            grouped[name, 0] = dst
+            if name == "g0":
+                interleave(engine, dst[:], w_raw[name][:])
+            else:
+                copy_on(engine, dst[:].rearrange("p (t m) j -> p t m j", t=PACK),
+                        w_raw[name][:].rearrange("p j (m t) -> p t m j", t=PACK))
+
+        def quantize(kind, c, pool):
+            cd = pool.tile([P, S], U32, name="codes_" + kind, align_bytes=64)
+            sc = pool.tile([P, S], U8, name="scales_" + kind, align_bytes=64)
+            codes[kind, c], scales[kind, c] = cd, sc
+            nc.vector.quantize_mx(out=cd[:].bitcast(FP8X4), scales=sc[:],
+                                  in_=grouped[kind, c][:].rearrange("p n t -> p (n t)"))
+
+        def mx(out, lhs, lhs_cols, rhs, rhs_cols, start, stop):
+            nc.tensor.matmul_mx(out=out, lhsT=codes[lhs][:, lhs_cols].bitcast(FP8X4), lhsT_scale=scales[lhs][:, lhs_cols],
+                                rhs=codes[rhs][:, rhs_cols].bitcast(FP8X4), rhs_scale=scales[rhs][:, rhs_cols],
+                                start=start, stop=stop)
+
+        def block(b):
+            return slice(P * b, P * (b + 1))
+
+        def scale_rows(c):
+            scaled[c] = work.tile([P, PACK, S], BF16, name="scaled", align_bytes=64)
+            for j in range(PACK):
+                nc.vector.tensor_scalar(out=scaled[c][:, j, :], in0=x_sb[c][:, j, :], scalar1=a_sb[:, 1, j : j + 1],
+                                        scalar2=None, op0=MULT)
+
+        def group_xh(c):
+            interleave("act", new_grouped("xh", c)[:], scaled[c][:])
+
+        def turn_x(c):
+            words = x_sb[c][:].bitcast(F32)
+            for jh in range(2):
+                bank = psum.tile([P, 2, 2, P], F32, name="turn", bufs=2)
+                banks["xw", c, jh] = bank
+                for u in range(2):
+                    for jj in range(2):
+                        nc.tensor.transpose(bank[:, u, jj, :], words[:, 2 * jh + jj, u : 2 * P : 2], ident[:])
+
+        def group_xw(c):
+            dst = new_grouped("xw", c)
+            factor = a_sb[:, 0, :].rearrange("p (u e) -> p u e", e=2).unsqueeze(1).to_broadcast([P, 2 * P, 2, 2])
+            for jh in range(2):
+                src = banks["xw", c, jh][:].rearrange("p u j r -> p (u j r)").bitcast(BF16)
+                nc.vector.tensor_tensor(
+                    out=dst[:, 2 * P * jh : 2 * P * (jh + 1), :].rearrange("p n (u e) -> p n u e", e=2),
+                    in0=src.rearrange("p (u n e) -> p n u e", u=2, e=2), in1=factor, op=MULT)
+
+        def stage1(c, k):
+            q, b = divmod(k, 4)
+            bank = psum.tile([P, PACK, P], F32, name="modes", bufs=4)
+            banks["u", c, k] = bank
+            for t in range(PACK):
+                mx(bank[:, t, :], (("f0", "f1")[q], 0), block(t), (("xw", "xh")[q], c), block(b), True, True)
+
+        def weigh(c, k):
+            q, b = divmod(k, 4)
+            kind = ("vw", "vh")[q]
+            if (kind, c) not in grouped:
+                new_grouped(kind, c)
+            dst = grouped[kind, c][:, block(b), :]
+            bank = banks["u", c, k]
+            if k >= 8 - ACT_BLOCKS[c]:
+                rows = work.tile([P, PACK, P], BF16, name="rows", align_bytes=64)
+                for t in range(PACK):
+                    nc.scalar.activation(out=rows[:, t, :], in_=bank[:, t, :], func=COPY,
+                                         scale=r_f32[:, q * C + c, t : t + 1])
+                interleave("act", dst, rows[:])
+            else:
+                factor = r_sb[:, q * C + c, :].unsqueeze(1).to_broadcast([P, P, PACK])
+                nc.vector.tensor_tensor(out=dst, in0=bank[:].rearrange("p t n -> p n t"), in1=factor, op=MULT)
+
+        def stage2(c, j):
+            bank = psum.tile([P, S], F32, name="field", bufs=2)
+            banks["y", c, j] = bank
+            mx(bank[:], ("vw", c), block(j), ("g0", 0), slice(0, S), True, False)
+            mx(bank[:], ("g1", 0), block(j), ("vh", c), slice(0, S), False, True)
+
+        def gelu(c, j):
+            if j == 0:
+                y_sb[c] = work.tile([P, PACK, S], F32, name="y_sb", align_bytes=64)
+                y_bf[c] = work.tile([P, PACK, S], BF16, name="y_bf", align_bytes=64)
+            bank = banks["y", c, j]
+            dst = y_bf[c][:, j, :].rearrange("p (u m e) -> p u m e", u=2, e=2)
+            nc.scalar.activation(out=y_sb[c][:, j, :], in_=bank[:], func=GELU)
+            if c < C - 1:
+                nc.scalar.activation(out=dst, in_=bank[:].rearrange("p (m u e) -> p u m e", u=2, e=2), func=GELU)
+            else:
+                nc.vector.tensor_copy(out=dst, in_=y_sb[c][:, j, :].rearrange("p (m u e) -> p u m e", u=2, e=2))
+                nc.sync.dma_start(out=out_0[c].rearrange("(p j) w -> p j w", j=PACK)[:, j, :], in_=y_sb[c][:, j, :])
+
+        def store_y(c):
+            if c < C - 1:
+                nc.sync.dma_start(out=out_0[c].rearrange("(p j) w -> p j w", j=PACK), in_=y_sb[c][:])
+
+        def turn_y(c, jh):
+            words = y_bf[c][:].bitcast(F32)
+            bank = psum.tile([P, 2, 2, P], F32, name="turn", bufs=2)
+            banks["pl", c, jh] = bank
+            for jj in range(2):
+                for u in range(2):
+                    nc.tensor.transpose(bank[:, jj, u, :], words[:, 2 * jh + jj, block(u)], ident[:])
+
+        def group_planes(c, jh):
+            if jh == 0:
+                new_grouped("pl", c)
+            dst = grouped["pl", c][:].rearrange("p n t -> p (n t)").bitcast(F32).rearrange("p (n k) -> p n k", k=8)
+            copy_on("act" if c < C - 1 else "dve", dst[:, :, 4 * jh : 4 * jh + 4],
+                    banks["pl", c, jh][:].rearrange("p j u n -> p n (j u)"))
+
+        def store_scales(cols):
+            for quad in range(4):
+                nc.sync.dma_start(out=scales_out[4 * quad : 4 * quad + 4, cols.start // 4 : cols.stop // 4],
+                                  in_=pl_scales[32 * quad : 32 * quad + 4, cols].bitcast(I32))
+
+        def planes(c):
+            cd = work.tile([P, S], U32, name="codes_pl", align_bytes=64)
+            cols = slice(S * c, S * (c + 1))
+            nc.vector.quantize_mx(out=cd[:].bitcast(FP8X4), scales=pl_scales[:, cols],
+                                  in_=grouped["pl", c][:].rearrange("p n t -> p (n t)"))
+            nc.sync.dma_start(out=words_out[:, cols], in_=cd[:].bitcast(I32))
+            if c == C - 2:
+                store_scales(slice(0, S * (C - 1)))
+            if c == C - 1:
+                store_scales(cols)
+
+        def live(c):
+            return 0 <= c < C
+
+        scale_rows(0)
+        group_xh(0)
+        turn_x(0)
+        group_weight("f0", "dve")
+        group_weight("f1", "act")
+        group_xw(0)
+        scale_rows(1)
+        quantize("f0", 0, keep)
+
+        for i in range(-1, C + 1):
+            nxt, far = i + 1, i + 2
+            if live(nxt):
+                quantize("xw", nxt, work)
+                for k in range(4):
+                    stage1(nxt, k)
+                quantize("xh", nxt, work)
+            if i == -1:
+                quantize("f1", 0, keep)
+            if live(far):
+                group_xh(far)
+                turn_x(far)
+            if i == -1:
+                group_weight("g0", "act")
+                group_weight("g1", "act")
+            if i == 0:
+                quantize("g0", 0, keep)
+                quantize("g1", 0, keep)
+            if live(i):
+                quantize("vw", i, work)
+                quantize("vh", i, work)
+                stage2(i, 0)
+                stage2(i, 1)
+            if live(i - 1):
+                planes(i - 1)
+            if live(i + 3):
+                scale_rows(i + 3)
+            if live(i):
+                gelu(i, 0)
+            if live(far):
+                group_xw(far)
+            if live(i):
+                stage2(i, 2)
+                gelu(i, 1)
+            if live(nxt):
+                weigh(nxt, 0)
+                stage1(nxt, 4)
+            if live(i):
+                stage2(i, 3)
+            if live(nxt):
+                weigh(nxt, 1)
+                stage1(nxt, 5)
+            if live(i):
+                gelu(i, 2)
+            if live(nxt):
+                weigh(nxt, 2)
+                stage1(nxt, 6)
+                weigh(nxt, 3)
+                stage1(nxt, 7)
+            if live(i):
+                gelu(i, 3)
+                store_y(i)
+                turn_y(i, 0)
+                turn_y(i, 1)
+            if live(nxt):
+                for k in range(4, 8):
+                    weigh(nxt, k)
+            if live(i):
+                group_planes(i, 0)
+                group_planes(i, 1)

@@ -18,7 +18,8 @@ P = 128
 PACK = 4
 FLOPS = 4 * 2 * C * S * S * S
 
-ACT_BLOCKS = (0, 1, 1, 1, 1, 1, 1, 2)
+POOL_PAIR = 9
+ACT_SCALE = 0
 
 
 def tile_factorizedtwoaxisspectraloperator_x1_kernel(tc, x, a, f, r, g, out_0, out_1, out_2):
@@ -37,7 +38,6 @@ def tile_factorizedtwoaxisspectraloperator_x1_kernel(tc, x, a, f, r, g, out_0, o
         warm = keep.tile([P, 2], F32, name="warm")
         nc.vector.memset(warm[:, 0:1], 0.0)
         warm_out = keep.tile([P, 1], F32, name="warm_out")
-        nc.scalar.activation(out=warm_out[:], in_=warm[:, 0:1], func=GELU)
 
         a_sb = keep.tile([P, 2, PACK], BF16, name="a_sb", align_bytes=64)
         r_sb = keep.tile([P, 2 * C, PACK], BF16, name="r_sb", align_bytes=64)
@@ -51,18 +51,26 @@ def tile_factorizedtwoaxisspectraloperator_x1_kernel(tc, x, a, f, r, g, out_0, o
         def load_rows(dst, src):
             nc.sync.dma_start(out=dst[:], in_=src.rearrange("(p j) n -> p j n", j=PACK))
 
-        nc.sync.dma_start(out=a_sb[:], in_=a.rearrange("q (p t) -> p q t", t=PACK))
-        load_rows(x_sb[0], x[0])
+        nc.scalar.dma_start(out=a_sb[:], in_=a.rearrange("q (p t) -> p q t", t=PACK))
+        r_rows = keep.tile([P, S], BF16, name="r_rows", align_bytes=64)
+        nc.vector.memset(r_rows[:], 0.0)
+        nc.scalar.dma_start(out=r_rows[0 : 2 * C, :], in_=r.rearrange("q c m -> (q c) m"))
+        nc.scalar.activation(out=warm_out[:], in_=warm[:, 0:1], func=GELU)
+        for jh in range(2):
+            nc.sync.dma_start(out=x_sb[0][:, 2 * jh : 2 * jh + 2, :],
+                              in_=x[0].rearrange("(p j) n -> p j n", j=PACK)[:, 2 * jh : 2 * jh + 2, :])
         load_rows(w_raw["f0"], w_hbm["f0"])
         load_rows(w_raw["f1"], w_hbm["f1"])
         load_rows(x_sb[1], x[1])
-        nc.sync.dma_start(out=r_sb[:], in_=r.rearrange("q c (p t) -> p (q c) t", t=PACK))
         load_rows(w_raw["g0"], w_hbm["g0"])
         load_rows(x_sb[2], x[2])
         load_rows(w_raw["g1"], w_hbm["g1"])
         for c in range(3, C):
             load_rows(x_sb[c], x[c])
-        nc.gpsimd.tensor_copy(out=r_f32[:], in_=r_sb[:])
+        if ACT_SCALE:
+            a_f32 = keep.tile([P, 2, PACK], F32, name="a_f32", align_bytes=64)
+            nc.vector.tensor_copy(out=a_f32[:], in_=a_sb[:])
+
 
         grouped = {}
         codes = {}
@@ -71,6 +79,7 @@ def tile_factorizedtwoaxisspectraloperator_x1_kernel(tc, x, a, f, r, g, out_0, o
         scaled = {}
         y_sb = {}
         y_bf = {}
+        rows = {}
 
         def new_grouped(kind, c):
             grouped[kind, c] = work.tile([P, S, PACK], BF16, name="grp_" + kind, align_bytes=64)
@@ -84,6 +93,10 @@ def tile_factorizedtwoaxisspectraloperator_x1_kernel(tc, x, a, f, r, g, out_0, o
 
         def interleave(engine, dst, src):
             copy_on(engine, dst.rearrange("p (c i) t -> p c t i", i=4), src.rearrange("p t (c i) -> p c t i", i=4))
+
+        def pool_interleave(dst, src):
+            nc.gpsimd.tensor_scalar(out=dst, in0=src.rearrange("p t n -> p n t"), scalar1=1.0, scalar2=1.0,
+                                    op0=MULT, op1=MULT)
 
         def group_weight(name, engine):
             dst = work.tile([P, S, PACK], BF16, name="grp_weight", align_bytes=64)
@@ -101,6 +114,13 @@ def tile_factorizedtwoaxisspectraloperator_x1_kernel(tc, x, a, f, r, g, out_0, o
             nc.vector.quantize_mx(out=cd[:].bitcast(FP8X4), scales=sc[:],
                                   in_=grouped[kind, c][:].rearrange("p n t -> p (n t)"))
 
+        def quantize_block(kind, c, b):
+            if b == 0:
+                codes[kind, c] = work.tile([P, S], U32, name="codes_" + kind, align_bytes=64)
+                scales[kind, c] = work.tile([P, S], U8, name="scales_" + kind, align_bytes=64)
+            nc.vector.quantize_mx(out=codes[kind, c][:, block(b)].bitcast(FP8X4), scales=scales[kind, c][:, block(b)],
+                                  in_=grouped[kind, c][:, block(b), :].rearrange("p n t -> p (n t)"))
+
         def mx(out, lhs, lhs_cols, rhs, rhs_cols, start, stop):
             nc.tensor.matmul_mx(out=out, lhsT=codes[lhs][:, lhs_cols].bitcast(FP8X4), lhsT_scale=scales[lhs][:, lhs_cols],
                                 rhs=codes[rhs][:, rhs_cols].bitcast(FP8X4), rhs_scale=scales[rhs][:, rhs_cols],
@@ -110,13 +130,21 @@ def tile_factorizedtwoaxisspectraloperator_x1_kernel(tc, x, a, f, r, g, out_0, o
             return slice(P * b, P * (b + 1))
 
         def scale_rows(c):
-            scaled[c] = work.tile([P, PACK, S], BF16, name="scaled", align_bytes=64)
-            for j in range(PACK):
+            for j in range(PACK - (ACT_SCALE if c > 1 else 0)):
                 nc.vector.tensor_scalar(out=scaled[c][:, j, :], in0=x_sb[c][:, j, :], scalar1=a_sb[:, 1, j : j + 1],
                                         scalar2=None, op0=MULT)
 
+        def scale_rows_act(c):
+            scaled[c] = work.tile([P, PACK, S], BF16, name="scaled", align_bytes=64)
+            for j in range(PACK - (ACT_SCALE if c > 1 else 0), PACK):
+                nc.scalar.activation(out=scaled[c][:, j, :], in_=x_sb[c][:, j, :], func=COPY, scale=a_f32[:, 1, j : j + 1])
+
         def group_xh(c):
-            interleave("act", new_grouped("xh", c)[:], scaled[c][:])
+            grouped["xh", c] = work.tile([P, S, PACK], BF16, name="grp_xh", align_bytes=64, bufs=1)
+            if c == 0:
+                interleave("act", grouped["xh", c][:], scaled[c][:])
+            else:
+                pool_interleave(grouped["xh", c][:], scaled[c][:])
 
         def turn_x(c):
             words = x_sb[c][:].bitcast(F32)
@@ -143,6 +171,27 @@ def tile_factorizedtwoaxisspectraloperator_x1_kernel(tc, x, a, f, r, g, out_0, o
             for t in range(PACK):
                 mx(bank[:, t, :], (("f0", "f1")[q], 0), block(t), (("xw", "xh")[q], c), block(b), True, True)
 
+        def stage1_pair(c):
+            for th in range(2):
+                bank = psum.tile([P, 2, 2 * P], F32, name="modes", bufs=4)
+                banks["pair", c, th] = bank
+                for tt in range(2):
+                    mx(bank[:, tt, :], ("f0", 0), block(2 * th + tt), ("xw", c), slice(0, 2 * P), True, True)
+
+        def weigh_pair(c):
+            new_grouped("vw", c)
+            rows[c] = work.tile([P, PACK, 2 * P], BF16, name="rows", align_bytes=64)
+            for t in range(PACK):
+                nc.scalar.activation(out=rows[c][:, t, :], in_=banks["pair", c, t // 2][:, t % 2, :], func=COPY,
+                                     scale=r_f32[:, c, t : t + 1])
+
+        def group_pair(c):
+            dst = grouped["vw", c][:, 0 : 2 * P, :]
+            if c >= POOL_PAIR:
+                pool_interleave(dst, rows[c][:])
+            else:
+                interleave("act", dst, rows[c][:])
+
         def weigh(c, k):
             q, b = divmod(k, 4)
             kind = ("vw", "vh")[q]
@@ -150,15 +199,8 @@ def tile_factorizedtwoaxisspectraloperator_x1_kernel(tc, x, a, f, r, g, out_0, o
                 new_grouped(kind, c)
             dst = grouped[kind, c][:, block(b), :]
             bank = banks["u", c, k]
-            if k >= 8 - ACT_BLOCKS[c]:
-                rows = work.tile([P, PACK, P], BF16, name="rows", align_bytes=64)
-                for t in range(PACK):
-                    nc.scalar.activation(out=rows[:, t, :], in_=bank[:, t, :], func=COPY,
-                                         scale=r_f32[:, q * C + c, t : t + 1])
-                interleave("act", dst, rows[:])
-            else:
-                factor = r_sb[:, q * C + c, :].unsqueeze(1).to_broadcast([P, P, PACK])
-                nc.vector.tensor_tensor(out=dst, in0=bank[:].rearrange("p t n -> p n t"), in1=factor, op=MULT)
+            factor = r_sb[:, q * C + c, :].unsqueeze(1).to_broadcast([P, P, PACK])
+            nc.vector.tensor_tensor(out=dst, in0=bank[:].rearrange("p t n -> p n t"), in1=factor, op=MULT)
 
         def stage2(c, j):
             bank = psum.tile([P, S], F32, name="field", bufs=2)
@@ -166,22 +208,27 @@ def tile_factorizedtwoaxisspectraloperator_x1_kernel(tc, x, a, f, r, g, out_0, o
             mx(bank[:], ("vw", c), block(j), ("g0", 0), slice(0, S), True, False)
             mx(bank[:], ("g1", 0), block(j), ("vh", c), slice(0, S), False, True)
 
-        def gelu(c, j):
-            if j == 0:
-                y_sb[c] = work.tile([P, PACK, S], F32, name="y_sb", align_bytes=64)
-                y_bf[c] = work.tile([P, PACK, S], BF16, name="y_bf", align_bytes=64)
-            bank = banks["y", c, j]
-            dst = y_bf[c][:, j, :].rearrange("p (u m e) -> p u m e", u=2, e=2)
-            nc.scalar.activation(out=y_sb[c][:, j, :], in_=bank[:], func=GELU)
-            if c < C - 1:
-                nc.scalar.activation(out=dst, in_=bank[:].rearrange("p (m u e) -> p u m e", u=2, e=2), func=GELU)
-            else:
-                nc.vector.tensor_copy(out=dst, in_=y_sb[c][:, j, :].rearrange("p (m u e) -> p u m e", u=2, e=2))
-                nc.sync.dma_start(out=out_0[c].rearrange("(p j) w -> p j w", j=PACK)[:, j, :], in_=y_sb[c][:, j, :])
+        def y_tiles(c):
+            y_sb[c] = work.tile([P, PACK, S], F32, name="y_sb", align_bytes=64)
+            y_bf[c] = work.tile([P, PACK, S], BF16, name="y_bf", align_bytes=64)
 
-        def store_y(c):
-            if c < C - 1:
-                nc.sync.dma_start(out=out_0[c].rearrange("(p j) w -> p j w", j=PACK), in_=y_sb[c][:])
+        def gelu_f32(c, j):
+            nc.scalar.activation(out=y_sb[c][:, j, :], in_=banks["y", c, j][:], func=GELU)
+
+        def gelu_bf16(c, j):
+            nc.scalar.activation(out=y_bf[c][:, j, :].rearrange("p (u m e) -> p u m e", u=2, e=2),
+                                 in_=banks["y", c, j][:].rearrange("p (m u e) -> p u m e", u=2, e=2), func=GELU)
+
+        def round_y(c, j):
+            nc.vector.tensor_copy(out=y_bf[c][:, j, :].rearrange("p (u m e) -> p u m e", u=2, e=2),
+                                  in_=y_sb[c][:, j, :].rearrange("p (m u e) -> p u m e", u=2, e=2))
+
+        def gelu(c, j):
+            gelu_f32(c, j)
+            gelu_bf16(c, j)
+
+        def store_y(c, js):
+            nc.sync.dma_start(out=out_0[c].rearrange("(p j) w -> p j w", j=PACK)[:, js, :], in_=y_sb[c][:, js, :])
 
         def turn_y(c, jh):
             words = y_bf[c][:].bitcast(F32)
@@ -191,16 +238,17 @@ def tile_factorizedtwoaxisspectraloperator_x1_kernel(tc, x, a, f, r, g, out_0, o
                 for u in range(2):
                     nc.tensor.transpose(bank[:, jj, u, :], words[:, 2 * jh + jj, block(u)], ident[:])
 
-        def group_planes(c, jh):
+        def group_planes(c, jh, engine):
             if jh == 0:
                 new_grouped("pl", c)
             dst = grouped["pl", c][:].rearrange("p n t -> p (n t)").bitcast(F32).rearrange("p (n k) -> p n k", k=8)
-            copy_on("act" if c < C - 1 else "dve", dst[:, :, 4 * jh : 4 * jh + 4],
+            copy_on(engine, dst[:, :, 4 * jh : 4 * jh + 4],
                     banks["pl", c, jh][:].rearrange("p j u n -> p n (j u)"))
 
         def store_scales(cols):
             for quad in range(4):
-                nc.sync.dma_start(out=scales_out[4 * quad : 4 * quad + 4, cols.start // 4 : cols.stop // 4],
+                queue = nc.scalar if cols.stop == C * S and quad % 2 else nc.sync
+                queue.dma_start(out=scales_out[4 * quad : 4 * quad + 4, cols.start // 4 : cols.stop // 4],
                                   in_=pl_scales[32 * quad : 32 * quad + 4, cols].bitcast(I32))
 
         def planes(c):
@@ -209,80 +257,159 @@ def tile_factorizedtwoaxisspectraloperator_x1_kernel(tc, x, a, f, r, g, out_0, o
             nc.vector.quantize_mx(out=cd[:].bitcast(FP8X4), scales=pl_scales[:, cols],
                                   in_=grouped["pl", c][:].rearrange("p n t -> p (n t)"))
             nc.sync.dma_start(out=words_out[:, cols], in_=cd[:].bitcast(I32))
-            if c == C - 2:
-                store_scales(slice(0, S * (C - 1)))
+            if c == C - 3:
+                store_scales(slice(0, S * (C - 2)))
             if c == C - 1:
-                store_scales(cols)
+                store_scales(slice(S * (C - 2), S * C))
 
         def live(c):
             return 0 <= c < C
 
+        scale_rows_act(0)
         scale_rows(0)
         group_xh(0)
         turn_x(0)
-        group_weight("f0", "dve")
-        group_weight("f1", "act")
         group_xw(0)
-        scale_rows(1)
-        quantize("f0", 0, keep)
+        r_bank = psum.tile([P, 2, 2, P], F32, name="turn", bufs=2)
+        for u in range(2):
+            nc.tensor.transpose(r_bank[:, u, 0, :], r_rows[:].bitcast(F32)[:, u : 2 * P : 2], ident[:])
+        group_weight("f0", "dve")
+        nc.vector.tensor_copy(out=r_sb[:].bitcast(F32), in_=r_bank[:, :, 0, 0 : 2 * C].rearrange("p u n -> p n u"))
+        group_weight("f1", "act")
+        nc.scalar.copy(out=r_f32[:], in_=r_sb[:])
+        scale_rows_act(1)
 
-        for i in range(-1, C + 1):
+        for i in range(-1, C - 2):
             nxt, far = i + 1, i + 2
-            if live(nxt):
-                quantize("xw", nxt, work)
-                for k in range(4):
-                    stage1(nxt, k)
-                quantize("xh", nxt, work)
+            todo = [2, 3, 4, 5, 6, 7]
+            quantize("xw", nxt, work)
             if i == -1:
-                quantize("f1", 0, keep)
-            if live(far):
-                group_xh(far)
-                turn_x(far)
-            if i == -1:
-                group_weight("g0", "act")
-                group_weight("g1", "act")
+                quantize("f0", 0, keep)
+            stage1_pair(nxt)
+            weigh_pair(nxt)
+            stage1(nxt, 2)
+            stage1(nxt, 3)
             if i == 0:
                 quantize("g0", 0, keep)
-                quantize("g1", 0, keep)
             if live(i):
                 quantize("vw", i, work)
                 quantize("vh", i, work)
+            if i == 0:
+                quantize("g1", 0, keep)
+            if live(i):
+                y_tiles(i)
                 stage2(i, 0)
                 stage2(i, 1)
+            if live(far):
+                turn_x(far)
+                scale_rows(far)
             if live(i - 1):
                 planes(i - 1)
-            if live(i + 3):
-                scale_rows(i + 3)
+            if i == -1:
+                weigh(nxt, 2)
+                weigh(nxt, 3)
+                quantize("f1", 0, keep)
+            quantize("xh", nxt, work)
+            stage1(nxt, 4)
+            stage1(nxt, 5)
+            if live(far):
+                group_xh(far)
             if live(i):
-                gelu(i, 0)
+                gelu_f32(i, 0)
+            group_pair(nxt)
+            if i == -1:
+                group_weight("g0", "act")
+                group_weight("g1", "act")
+            if live(i):
+                gelu_bf16(i, 0)
+                stage2(i, 2)
+            if i >= 0:
+                weigh(nxt, 2)
+            stage1(nxt, 6)
+            if i >= 0:
+                weigh(nxt, 3)
+            stage1(nxt, 7)
             if live(far):
                 group_xw(far)
             if live(i):
-                stage2(i, 2)
                 gelu(i, 1)
-            if live(nxt):
-                weigh(nxt, 0)
-                stage1(nxt, 4)
-            if live(i):
                 stage2(i, 3)
-            if live(nxt):
-                weigh(nxt, 1)
-                stage1(nxt, 5)
+                turn_y(i, 0)
+            weigh(nxt, 4)
+            weigh(nxt, 5)
             if live(i):
                 gelu(i, 2)
-            if live(nxt):
-                weigh(nxt, 2)
-                stage1(nxt, 6)
-                weigh(nxt, 3)
-                stage1(nxt, 7)
-            if live(i):
                 gelu(i, 3)
-                store_y(i)
-                turn_y(i, 0)
+                store_y(i, slice(0, 4))
                 turn_y(i, 1)
-            if live(nxt):
-                for k in range(4, 8):
-                    weigh(nxt, k)
+            weigh(nxt, 6)
+            weigh(nxt, 7)
             if live(i):
-                group_planes(i, 0)
-                group_planes(i, 1)
+                group_planes(i, 0, "act")
+            if live(i + 3):
+                scale_rows_act(i + 3)
+            if live(i):
+                group_planes(i, 1, "act")
+
+        prev, last = C - 2, C - 1
+        quantize("xh", last, work)
+        for k in range(4, 8):
+            stage1(last, k)
+        quantize("vw", prev, work)
+        quantize("vh", prev, work)
+        y_tiles(prev)
+        stage2(prev, 0)
+        stage2(prev, 1)
+        quantize("xw", last, work)
+        planes(prev - 1)
+        weigh(last, 4)
+        stage1(last, 0)
+        gelu(prev, 0)
+        stage2(prev, 2)
+        weigh(last, 5)
+        stage1(last, 1)
+        weigh(last, 6)
+        stage1(last, 2)
+        gelu(prev, 1)
+        stage2(prev, 3)
+        turn_y(prev, 0)
+        weigh(last, 7)
+        stage1(last, 3)
+        weigh(last, 0)
+        quantize("vh", last, work)
+        quantize_block("vw", last, 0)
+        gelu(prev, 2)
+        gelu(prev, 3)
+        store_y(prev, slice(0, 4))
+        y_tiles(last)
+        stage2(last, 0)
+        turn_y(prev, 1)
+        group_planes(prev, 0, "act")
+        weigh(last, 1)
+        weigh(last, 2)
+        quantize_block("vw", last, 1)
+        stage2(last, 1)
+        gelu_f32(last, 0)
+        store_y(last, slice(0, 1))
+        weigh(last, 3)
+        quantize_block("vw", last, 2)
+        stage2(last, 2)
+        group_planes(prev, 1, "dve")
+        quantize_block("vw", last, 3)
+        gelu_f32(last, 1)
+        store_y(last, slice(1, 2))
+        stage2(last, 3)
+        round_y(last, 0)
+        round_y(last, 1)
+        turn_y(last, 0)
+        planes(prev)
+        gelu_f32(last, 2)
+        store_y(last, slice(2, 3))
+        gelu_bf16(last, 3)
+        round_y(last, 2)
+        turn_y(last, 1)
+        gelu_f32(last, 3)
+        store_y(last, slice(3, 4))
+        group_planes(last, 0, "act")
+        group_planes(last, 1, "dve")
+        planes(last)

@@ -13,13 +13,33 @@ MULT = mybir.AluOpType.mult
 GELU = mybir.ActivationFunctionType.Gelu_apprx_tanh
 COPY = mybir.ActivationFunctionType.Copy
 
-C, S = 8, 512
+C = 8
+S = 512
 P = 128
 PACK = 4
+HALF = S // 2
+ALIGN = 64
 FLOPS = 4 * 2 * C * S * S * S
 
-POOL_PAIR = 9
-ACT_SCALE = 0
+TURN_BANKS, MODE_BANKS, FIELD_BANKS = 2, 4, 2
+
+WARM_BEFORE, WARM_BETWEEN, WARM_AFTER, WARM_STEP = 12, 10, 5, 2
+
+
+def block(b):
+    return slice(P * b, P * (b + 1))
+
+
+def half(h):
+    return slice(HALF * h, HALF * (h + 1))
+
+
+def by_slots(rows):
+    return rows.rearrange("(p j) n -> p j n", j=PACK)
+
+
+def flat(grouped_tile):
+    return grouped_tile.rearrange("p n t -> p (n t)")
 
 
 def tile_factorizedtwoaxisspectraloperator_x1_kernel(tc, x, a, f, r, g, out_0, out_1, out_2):
@@ -33,383 +53,409 @@ def tile_factorizedtwoaxisspectraloperator_x1_kernel(tc, x, a, f, r, g, out_0, o
         psum = ctx.enter_context(tc.psum_pool(name="psum", bufs=2))
         ctx.enter_context(tc.manual_schedule())
 
-        ident = keep.tile([P, P], F32, name="ident", align_bytes=64)
+        ident = keep.tile([P, P], F32, name="ident", align_bytes=ALIGN)
         make_identity(nc, ident[:])
-        warm = keep.tile([P, 2], F32, name="warm")
-        nc.vector.memset(warm[:, 0:1], 0.0)
-        warm_out = keep.tile([P, 1], F32, name="warm_out")
 
-        a_sb = keep.tile([P, 2, PACK], BF16, name="a_sb", align_bytes=64)
-        r_sb = keep.tile([P, 2 * C, PACK], BF16, name="r_sb", align_bytes=64)
-        r_f32 = keep.tile([P, 2 * C, PACK], F32, name="r_f32", align_bytes=64)
-        x_sb = [keep.tile([P, PACK, S], BF16, name="x_sb%d" % c, align_bytes=64) for c in range(C)]
-        w_names = ("f0", "f1", "g0", "g1")
+        a_sb = keep.tile([P, 2, PACK], BF16, name="a_sb", align_bytes=ALIGN)
+        r_rows = keep.tile([P, S], BF16, name="r_rows", align_bytes=ALIGN)
+        r_sb = keep.tile([P, 2 * C, PACK], BF16, name="r_sb", align_bytes=ALIGN)
+        r0_f32 = keep.tile([P, C, PACK], F32, name="r0_f32", align_bytes=ALIGN)
+        x_sb = [keep.tile([P, PACK, S], BF16, name="x_sb%d" % c, align_bytes=ALIGN) for c in range(C)]
         w_hbm = {"f0": f[0], "f1": f[1], "g0": g[0], "g1": g[1]}
-        w_raw = {n: keep.tile([P, PACK, S], BF16, name="raw_" + n, align_bytes=64) for n in w_names}
-        pl_scales = keep.tile([P, C * S], U8, name="pl_scales", align_bytes=64)
-
-        def load_rows(dst, src):
-            nc.sync.dma_start(out=dst[:], in_=src.rearrange("(p j) n -> p j n", j=PACK))
+        w_sb = {w: keep.tile([P, PACK, S], BF16, name="raw_" + w, align_bytes=ALIGN) for w in w_hbm}
+        out_scales = keep.tile([P, C * S], U8, name="out_scales", align_bytes=ALIGN)
+        idle_codes = keep.tile([P, P], U32, name="idle_codes", align_bytes=ALIGN)
+        idle_scales = keep.tile([P, P], U8, name="idle_scales", align_bytes=ALIGN)
+        table_warm = keep.tile([P, 1], F32, name="table_warm")
 
         nc.scalar.dma_start(out=a_sb[:], in_=a.rearrange("q (p t) -> p q t", t=PACK))
-        r_rows = keep.tile([P, S], BF16, name="r_rows", align_bytes=64)
         nc.vector.memset(r_rows[:], 0.0)
-        nc.scalar.dma_start(out=r_rows[0 : 2 * C, :], in_=r.rearrange("q c m -> (q c) m"))
-        nc.scalar.activation(out=warm_out[:], in_=warm[:, 0:1], func=GELU)
+        nc.vector.quantize_mx(out=idle_codes[:].bitcast(FP8X4), scales=idle_scales[:], in_=r_rows[:])
+        nc.scalar.activation(out=table_warm[:], in_=ident[:, 0:1], func=GELU)
+
         for jh in range(2):
-            nc.sync.dma_start(out=x_sb[0][:, 2 * jh : 2 * jh + 2, :],
-                              in_=x[0].rearrange("(p j) n -> p j n", j=PACK)[:, 2 * jh : 2 * jh + 2, :])
-        load_rows(w_raw["f0"], w_hbm["f0"])
-        load_rows(w_raw["f1"], w_hbm["f1"])
-        load_rows(x_sb[1], x[1])
-        load_rows(w_raw["g0"], w_hbm["g0"])
-        load_rows(x_sb[2], x[2])
-        load_rows(w_raw["g1"], w_hbm["g1"])
-        for c in range(3, C):
-            load_rows(x_sb[c], x[c])
-        if ACT_SCALE:
-            a_f32 = keep.tile([P, 2, PACK], F32, name="a_f32", align_bytes=64)
-            nc.vector.tensor_copy(out=a_f32[:], in_=a_sb[:])
+            slots = slice(2 * jh, 2 * jh + 2)
+            nc.sync.dma_start(out=x_sb[0][:, slots, :], in_=by_slots(x[0])[:, slots, :])
+        nc.sync.dma_start(out=w_sb["f0"][:], in_=by_slots(w_hbm["f0"]))
+        nc.sync.dma_start(out=r_rows[0 : 2 * C, :], in_=r.rearrange("q c m -> (q c) m"))
+        for dst, src in (
+            [(w_sb["f1"], w_hbm["f1"]), (x_sb[1], x[1])]
+            + [(w_sb["g0"], w_hbm["g0"]), (x_sb[2], x[2]), (w_sb["g1"], w_hbm["g1"])]
+            + [(x_sb[c], x[c]) for c in range(3, C)]
+        ):
+            nc.sync.dma_start(out=dst[:], in_=by_slots(src))
+
+        grouped, codes, scales, banks, staged = {}, {}, {}, {}, {}
+
+        def stage_tile(name, c, shape, dtype, bufs=2):
+            if (name, c) not in staged:
+                staged[name, c] = work.tile(shape, dtype, name=name, align_bytes=ALIGN, bufs=bufs)
+            return staged[name, c]
+
+        def modes_tile(c):
+            return stage_tile("grouped_v", c, [P, 2 * S, PACK], BF16)
+
+        def field_bank(c, j):
+            if ("y", c, j) not in banks:
+                if c == C - 1 and j % 2:
+                    banks["y", c, j] = psum.tile([P, S], F32, name="modes", bufs=MODE_BANKS)
+                else:
+                    banks["y", c, j] = psum.tile([P, S], F32, name="field", bufs=FIELD_BANKS)
+            return banks["y", c, j]
+
+        def interleave_on_scalar(dst, src):
+            nc.scalar.copy(out=dst.rearrange("p (n i) t -> p n t i", i=4), in_=src.rearrange("p t (n i) -> p n t i", i=4))
+
+        def quantize_into(name, grouped_ap, pool):
+            width = grouped_ap.shape[1]
+            tag = name[0]
+            codes[name] = pool.tile([P, width], U32, name="codes_" + tag, align_bytes=ALIGN)
+            scales[name] = pool.tile([P, width], U8, name="scales_" + tag, align_bytes=ALIGN)
+            nc.vector.quantize_mx(out=codes[name][:].bitcast(FP8X4), scales=scales[name][:], in_=flat(grouped_ap))
+
+        def mx(out, lhs, lhs_cols, rhs, rhs_cols, start=True, stop=True):
+            nc.tensor.matmul_mx(
+                out=out,
+                lhsT=codes[lhs][:, lhs_cols].bitcast(FP8X4),
+                lhsT_scale=scales[lhs][:, lhs_cols],
+                rhs=codes[rhs][:, rhs_cols].bitcast(FP8X4),
+                rhs_scale=scales[rhs][:, rhs_cols],
+                start=start,
+                stop=stop,
+            )
 
 
-        grouped = {}
-        codes = {}
-        scales = {}
-        banks = {}
-        scaled = {}
-        y_sb = {}
-        y_bf = {}
-        rows = {}
-
-        def new_grouped(kind, c):
-            grouped[kind, c] = work.tile([P, S, PACK], BF16, name="grp_" + kind, align_bytes=64)
-            return grouped[kind, c]
-
-        def copy_on(engine, out, in_):
-            if engine == "act":
-                nc.scalar.copy(out=out, in_=in_)
+        def group_weight(w, copy):
+            grouped[w] = work.tile([P, S, PACK], BF16, name="grouped_weight", align_bytes=ALIGN)
+            if w == "g0":
+                interleave_on_scalar(grouped[w][:], w_sb[w][:])
             else:
-                nc.vector.tensor_copy(out=out, in_=in_)
+                copy(
+                    out=grouped[w][:].rearrange("p (t i) j -> p t i j", t=PACK),
+                    in_=w_sb[w][:].rearrange("p j (i t) -> p t i j", t=PACK),
+                )
 
-        def interleave(engine, dst, src):
-            copy_on(engine, dst.rearrange("p (c i) t -> p c t i", i=4), src.rearrange("p t (c i) -> p c t i", i=4))
+        def quantize_weight(w):
+            quantize_into((w,), grouped[w][:], keep)
 
-        def pool_interleave(dst, src):
-            nc.gpsimd.tensor_scalar(out=dst, in0=src.rearrange("p t n -> p n t"), scalar1=1.0, scalar2=1.0,
-                                    op0=MULT, op1=MULT)
+        def turn_r():
+            banks["r"] = psum.tile([P, 2, P], F32, name="turn", bufs=TURN_BANKS)
+            for u in range(2):
+                nc.tensor.transpose(banks["r"][:, u, :], r_rows[:].bitcast(F32)[:, u : 2 * P : 2], ident[:])
 
-        def group_weight(name, engine):
-            dst = work.tile([P, S, PACK], BF16, name="grp_weight", align_bytes=64)
-            grouped[name, 0] = dst
-            if name == "g0":
-                interleave(engine, dst[:], w_raw[name][:])
-            else:
-                copy_on(engine, dst[:].rearrange("p (t m) j -> p t m j", t=PACK),
-                        w_raw[name][:].rearrange("p j (m t) -> p t m j", t=PACK))
+        def group_r():
+            nc.vector.tensor_copy(out=r_sb[:].bitcast(F32), in_=banks["r"][:, :, 0 : 2 * C].rearrange("p u n -> p n u"))
+            nc.scalar.copy(out=r0_f32[:], in_=r_sb[:, 0:C, :])
 
-        def quantize(kind, c, pool):
-            cd = pool.tile([P, S], U32, name="codes_" + kind, align_bytes=64)
-            sc = pool.tile([P, S], U8, name="scales_" + kind, align_bytes=64)
-            codes[kind, c], scales[kind, c] = cd, sc
-            nc.vector.quantize_mx(out=cd[:].bitcast(FP8X4), scales=sc[:],
-                                  in_=grouped[kind, c][:].rearrange("p n t -> p (n t)"))
+        def warm_on_zeros(passes):
+            codes["idle",], scales["idle",] = idle_codes, idle_scales
+            for k in range(passes):
+                mx(field_bank(0, 0)[:, block(k % PACK)], ("idle",), block(0), ("idle",), block(0))
 
-        def quantize_block(kind, c, b):
-            if b == 0:
-                codes[kind, c] = work.tile([P, S], U32, name="codes_" + kind, align_bytes=64)
-                scales[kind, c] = work.tile([P, S], U8, name="scales_" + kind, align_bytes=64)
-            nc.vector.quantize_mx(out=codes[kind, c][:, block(b)].bitcast(FP8X4), scales=scales[kind, c][:, block(b)],
-                                  in_=grouped[kind, c][:, block(b), :].rearrange("p n t -> p (n t)"))
+        def keep_warm(c, passes):
+            for k in range(passes):
+                mx(field_bank(c, 0)[:], ("f0",), block(0), ("f1",), slice(0, S))
 
-        def mx(out, lhs, lhs_cols, rhs, rhs_cols, start, stop):
-            nc.tensor.matmul_mx(out=out, lhsT=codes[lhs][:, lhs_cols].bitcast(FP8X4), lhsT_scale=scales[lhs][:, lhs_cols],
-                                rhs=codes[rhs][:, rhs_cols].bitcast(FP8X4), rhs_scale=scales[rhs][:, rhs_cols],
-                                start=start, stop=stop)
 
-        def block(b):
-            return slice(P * b, P * (b + 1))
-
-        def scale_rows(c):
-            for j in range(PACK - (ACT_SCALE if c > 1 else 0)):
-                nc.vector.tensor_scalar(out=scaled[c][:, j, :], in0=x_sb[c][:, j, :], scalar1=a_sb[:, 1, j : j + 1],
-                                        scalar2=None, op0=MULT)
-
-        def scale_rows_act(c):
-            scaled[c] = work.tile([P, PACK, S], BF16, name="scaled", align_bytes=64)
-            for j in range(PACK - (ACT_SCALE if c > 1 else 0), PACK):
-                nc.scalar.activation(out=scaled[c][:, j, :], in_=x_sb[c][:, j, :], func=COPY, scale=a_f32[:, 1, j : j + 1])
+        def scale_rows(c, slots):
+            scaled = stage_tile("scaled", c, [P, PACK, S], BF16)
+            for j in slots:
+                nc.vector.tensor_scalar(
+                    out=scaled[:, j, :], in0=x_sb[c][:, j, :], scalar1=a_sb[:, 1, j : j + 1], scalar2=None, op0=MULT
+                )
 
         def group_xh(c):
-            grouped["xh", c] = work.tile([P, S, PACK], BF16, name="grp_xh", align_bytes=64, bufs=1)
+            dst = stage_tile("grouped_xh", c, [P, S, PACK], BF16, bufs=1)
+            scaled = staged["scaled", c]
             if c == 0:
-                interleave("act", grouped["xh", c][:], scaled[c][:])
+                interleave_on_scalar(dst[:], scaled[:])
             else:
-                pool_interleave(grouped["xh", c][:], scaled[c][:])
+                nc.gpsimd.tensor_scalar(
+                    out=dst[:], in0=scaled[:].rearrange("p t n -> p n t"), scalar1=1.0, scalar2=1.0, op0=MULT, op1=MULT
+                )
 
-        def turn_x(c):
+        def turn_x(c, jh):
             words = x_sb[c][:].bitcast(F32)
-            for jh in range(2):
-                bank = psum.tile([P, 2, 2, P], F32, name="turn", bufs=2)
-                banks["xw", c, jh] = bank
-                for u in range(2):
-                    for jj in range(2):
-                        nc.tensor.transpose(bank[:, u, jj, :], words[:, 2 * jh + jj, u : 2 * P : 2], ident[:])
+            bank = psum.tile([P, 2, 2, P], F32, name="turn", bufs=TURN_BANKS)
+            banks["xw", c, jh] = bank
+            for u in range(2):
+                for jj in range(2):
+                    nc.tensor.transpose(bank[:, u, jj, :], words[:, 2 * jh + jj, u : 2 * P : 2], ident[:])
 
-        def group_xw(c):
-            dst = new_grouped("xw", c)
-            factor = a_sb[:, 0, :].rearrange("p (u e) -> p u e", e=2).unsqueeze(1).to_broadcast([P, 2 * P, 2, 2])
-            for jh in range(2):
-                src = banks["xw", c, jh][:].rearrange("p u j r -> p (u j r)").bitcast(BF16)
-                nc.vector.tensor_tensor(
-                    out=dst[:, 2 * P * jh : 2 * P * (jh + 1), :].rearrange("p n (u e) -> p n u e", e=2),
-                    in0=src.rearrange("p (u n e) -> p n u e", u=2, e=2), in1=factor, op=MULT)
+        def group_xw(c, jh):
+            dst = stage_tile("grouped_xw", c, [P, S, PACK], BF16)
+            src = banks["xw", c, jh][:].rearrange("p u j i -> p (u j i)").bitcast(BF16)
+            factor = a_sb[:, 0, :].rearrange("p (u e) -> p u e", e=2).unsqueeze(1).to_broadcast([P, HALF, 2, 2])
+            nc.vector.tensor_tensor(
+                out=dst[:, half(jh), :].rearrange("p n (u e) -> p n u e", e=2),
+                in0=src.rearrange("p (u n e) -> p n u e", u=2, e=2),
+                in1=factor,
+                op=MULT,
+            )
 
-        def stage1(c, k):
-            q, b = divmod(k, 4)
-            bank = psum.tile([P, PACK, P], F32, name="modes", bufs=4)
+        def quantize_x(kind, c):
+            quantize_into((kind, c), staged["grouped_" + kind, c][:], work)
+
+        def to_modes(c, k):
+            q, b = divmod(k, PACK)
+            bank = psum.tile([P, PACK, P], F32, name="modes", bufs=MODE_BANKS)
             banks["u", c, k] = bank
             for t in range(PACK):
-                mx(bank[:, t, :], (("f0", "f1")[q], 0), block(t), (("xw", "xh")[q], c), block(b), True, True)
-
-        def stage1_pair(c):
-            for th in range(2):
-                bank = psum.tile([P, 2, 2 * P], F32, name="modes", bufs=4)
-                banks["pair", c, th] = bank
-                for tt in range(2):
-                    mx(bank[:, tt, :], ("f0", 0), block(2 * th + tt), ("xw", c), slice(0, 2 * P), True, True)
-
-        def weigh_pair(c):
-            new_grouped("vw", c)
-            rows[c] = work.tile([P, PACK, 2 * P], BF16, name="rows", align_bytes=64)
-            for t in range(PACK):
-                nc.scalar.activation(out=rows[c][:, t, :], in_=banks["pair", c, t // 2][:, t % 2, :], func=COPY,
-                                     scale=r_f32[:, c, t : t + 1])
-
-        def group_pair(c):
-            dst = grouped["vw", c][:, 0 : 2 * P, :]
-            if c >= POOL_PAIR:
-                pool_interleave(dst, rows[c][:])
-            else:
-                interleave("act", dst, rows[c][:])
+                mx(bank[:, t, :], (("f0", "f1")[q],), block(t), (("xw", "xh")[q], c), block(b))
 
         def weigh(c, k):
-            q, b = divmod(k, 4)
-            kind = ("vw", "vh")[q]
-            if (kind, c) not in grouped:
-                new_grouped(kind, c)
-            dst = grouped[kind, c][:, block(b), :]
-            bank = banks["u", c, k]
-            factor = r_sb[:, q * C + c, :].unsqueeze(1).to_broadcast([P, P, PACK])
-            nc.vector.tensor_tensor(out=dst, in0=bank[:].rearrange("p t n -> p n t"), in1=factor, op=MULT)
+            factor = r_sb[:, C * (k // PACK) + c, :].unsqueeze(1).to_broadcast([P, P, PACK])
+            nc.vector.tensor_tensor(
+                out=modes_tile(c)[:, block(k), :], in0=banks["u", c, k][:].rearrange("p t n -> p n t"), in1=factor, op=MULT
+            )
 
-        def stage2(c, j):
-            bank = psum.tile([P, S], F32, name="field", bufs=2)
-            banks["y", c, j] = bank
-            mx(bank[:], ("vw", c), block(j), ("g0", 0), slice(0, S), True, False)
-            mx(bank[:], ("g1", 0), block(j), ("vh", c), slice(0, S), False, True)
+        def to_modes_wide(c, th):
+            bank = psum.tile([P, 2, HALF], F32, name="modes", bufs=MODE_BANKS)
+            banks["wide", c, th] = bank
+            for tt in range(2):
+                mx(bank[:, tt, :], ("f0",), block(2 * th + tt), ("xw", c), half(0))
 
-        def y_tiles(c):
-            y_sb[c] = work.tile([P, PACK, S], F32, name="y_sb", align_bytes=64)
-            y_bf[c] = work.tile([P, PACK, S], BF16, name="y_bf", align_bytes=64)
+        def weigh_wide(c, th):
+            weighed = stage_tile("weighed", c, [P, PACK, HALF], BF16)
+            for tt in range(2):
+                t = 2 * th + tt
+                nc.scalar.activation(
+                    out=weighed[:, t, :], in_=banks["wide", c, th][:, tt, :], func=COPY, scale=r0_f32[:, c, t : t + 1]
+                )
+
+        def group_wide(c):
+            interleave_on_scalar(modes_tile(c)[:, half(0), :], staged["weighed", c][:])
+
+        def quantize_modes(c):
+            quantize_into(("v", c), modes_tile(c)[:], work)
+
+        def quantize_modes_part(c, cols):
+            if ("v", c) not in codes:
+                codes["v", c] = work.tile([P, 2 * S], U32, name="codes_v", align_bytes=ALIGN)
+                scales["v", c] = work.tile([P, 2 * S], U8, name="scales_v", align_bytes=ALIGN)
+            nc.vector.quantize_mx(
+                out=codes["v", c][:, cols].bitcast(FP8X4), scales=scales["v", c][:, cols], in_=flat(modes_tile(c)[:, cols, :])
+            )
+
+        def to_field(c, j):
+            bank = field_bank(c, j)
+            mx(bank[:], ("v", c), block(j), ("g0",), slice(0, S), stop=False)
+            mx(bank[:], ("g1",), block(j), ("v", c), slice(S, 2 * S), start=False)
+
+        def by_words(row):
+            return row.rearrange("p (i u e) -> p u i e", u=2, e=2)
+
+        def y_f32(c):
+            return stage_tile("y_f32", c, [P, PACK, S], F32)
+
+        def y_bf16_slot(c, j):
+            return stage_tile("y_bf16", c, [P, PACK, S], BF16)[:, j, :].rearrange("p (u i e) -> p u i e", u=2, e=2)
 
         def gelu_f32(c, j):
-            nc.scalar.activation(out=y_sb[c][:, j, :], in_=banks["y", c, j][:], func=GELU)
+            nc.scalar.activation(out=y_f32(c)[:, j, :], in_=banks["y", c, j][:], func=GELU)
 
         def gelu_bf16(c, j):
-            nc.scalar.activation(out=y_bf[c][:, j, :].rearrange("p (u m e) -> p u m e", u=2, e=2),
-                                 in_=banks["y", c, j][:].rearrange("p (m u e) -> p u m e", u=2, e=2), func=GELU)
+            nc.scalar.activation(out=y_bf16_slot(c, j), in_=by_words(banks["y", c, j][:]), func=GELU)
 
         def round_y(c, j):
-            nc.vector.tensor_copy(out=y_bf[c][:, j, :].rearrange("p (u m e) -> p u m e", u=2, e=2),
-                                  in_=y_sb[c][:, j, :].rearrange("p (m u e) -> p u m e", u=2, e=2))
+            nc.vector.tensor_copy(out=y_bf16_slot(c, j), in_=by_words(y_f32(c)[:, j, :]))
 
-        def gelu(c, j):
-            gelu_f32(c, j)
-            gelu_bf16(c, j)
-
-        def store_y(c, js):
-            nc.sync.dma_start(out=out_0[c].rearrange("(p j) w -> p j w", j=PACK)[:, js, :], in_=y_sb[c][:, js, :])
+        def store_y(c, slots):
+            nc.sync.dma_start(out=by_slots(out_0[c])[:, slots, :], in_=y_f32(c)[:, slots, :])
 
         def turn_y(c, jh):
-            words = y_bf[c][:].bitcast(F32)
-            bank = psum.tile([P, 2, 2, P], F32, name="turn", bufs=2)
-            banks["pl", c, jh] = bank
+            words = staged["y_bf16", c][:].bitcast(F32)
+            bank = psum.tile([P, 2, 2, P], F32, name="turn", bufs=TURN_BANKS)
+            banks["out", c, jh] = bank
             for jj in range(2):
                 for u in range(2):
                     nc.tensor.transpose(bank[:, jj, u, :], words[:, 2 * jh + jj, block(u)], ident[:])
 
-        def group_planes(c, jh, engine):
-            if jh == 0:
-                new_grouped("pl", c)
-            dst = grouped["pl", c][:].rearrange("p n t -> p (n t)").bitcast(F32).rearrange("p (n k) -> p n k", k=8)
-            copy_on(engine, dst[:, :, 4 * jh : 4 * jh + 4],
-                    banks["pl", c, jh][:].rearrange("p j u n -> p n (j u)"))
+        def group_out(c, jh, copy, rows=slice(0, P)):
+            words = flat(stage_tile("grouped_out", c, [P, S, PACK], BF16)[:]).bitcast(F32)
+            copy(
+                out=words.rearrange("p (i k) -> p i k", k=8)[:, rows, 4 * jh : 4 * jh + 4],
+                in_=banks["out", c, jh][:].rearrange("p j u i -> p i (j u)")[:, rows, :],
+            )
 
-        def store_scales(cols):
+        def quantize_out(c, cols=slice(0, S)):
+            out_codes = work.tile([P, cols.stop - cols.start], U32, name="out_codes", align_bytes=ALIGN, bufs=3)
+            at = slice(S * c + cols.start, S * c + cols.stop)
+            nc.vector.quantize_mx(
+                out=out_codes[:].bitcast(FP8X4), scales=out_scales[:, at], in_=flat(staged["grouped_out", c][:, cols, :])
+            )
+            nc.sync.dma_start(out=words_out[:, at], in_=out_codes[:].bitcast(I32))
+
+        def store_scales(first, stop, queues):
             for quad in range(4):
-                queue = nc.scalar if cols.stop == C * S and quad % 2 else nc.sync
-                queue.dma_start(out=scales_out[4 * quad : 4 * quad + 4, cols.start // 4 : cols.stop // 4],
-                                  in_=pl_scales[32 * quad : 32 * quad + 4, cols].bitcast(I32))
+                queues[quad % 2].dma_start(
+                    out=scales_out[4 * quad : 4 * quad + 4, P * first : P * stop],
+                    in_=out_scales[32 * quad : 32 * quad + 4, S * first : S * stop].bitcast(I32),
+                )
 
-        def planes(c):
-            cd = work.tile([P, S], U32, name="codes_pl", align_bytes=64)
-            cols = slice(S * c, S * (c + 1))
-            nc.vector.quantize_mx(out=cd[:].bitcast(FP8X4), scales=pl_scales[:, cols],
-                                  in_=grouped["pl", c][:].rearrange("p n t -> p (n t)"))
-            nc.sync.dma_start(out=words_out[:, cols], in_=cd[:].bitcast(I32))
-            if c == C - 3:
-                store_scales(slice(0, S * (C - 2)))
-            if c == C - 1:
-                store_scales(slice(S * (C - 2), S * C))
+        on_scalar, on_vector = nc.scalar.copy, nc.vector.tensor_copy
 
-        def live(c):
-            return 0 <= c < C
-
-        scale_rows_act(0)
-        scale_rows(0)
+        warm_on_zeros(WARM_BEFORE)
+        scale_rows(0, range(PACK))
         group_xh(0)
-        turn_x(0)
-        group_xw(0)
-        r_bank = psum.tile([P, 2, 2, P], F32, name="turn", bufs=2)
-        for u in range(2):
-            nc.tensor.transpose(r_bank[:, u, 0, :], r_rows[:].bitcast(F32)[:, u : 2 * P : 2], ident[:])
-        group_weight("f0", "dve")
-        nc.vector.tensor_copy(out=r_sb[:].bitcast(F32), in_=r_bank[:, :, 0, 0 : 2 * C].rearrange("p u n -> p n u"))
-        group_weight("f1", "act")
-        nc.scalar.copy(out=r_f32[:], in_=r_sb[:])
-        scale_rows_act(1)
-
-        for i in range(-1, C - 2):
-            nxt, far = i + 1, i + 2
-            todo = [2, 3, 4, 5, 6, 7]
-            quantize("xw", nxt, work)
-            if i == -1:
-                quantize("f0", 0, keep)
-            stage1_pair(nxt)
-            weigh_pair(nxt)
-            stage1(nxt, 2)
-            stage1(nxt, 3)
-            if i == 0:
-                quantize("g0", 0, keep)
-            if live(i):
-                quantize("vw", i, work)
-                quantize("vh", i, work)
-            if i == 0:
-                quantize("g1", 0, keep)
-            if live(i):
-                y_tiles(i)
-                stage2(i, 0)
-                stage2(i, 1)
-            if live(far):
-                turn_x(far)
-                scale_rows(far)
-            if live(i - 1):
-                planes(i - 1)
-            if i == -1:
-                weigh(nxt, 2)
-                weigh(nxt, 3)
-                quantize("f1", 0, keep)
-            quantize("xh", nxt, work)
-            stage1(nxt, 4)
-            stage1(nxt, 5)
-            if live(far):
-                group_xh(far)
-            if live(i):
-                gelu_f32(i, 0)
-            group_pair(nxt)
-            if i == -1:
-                group_weight("g0", "act")
-                group_weight("g1", "act")
-            if live(i):
-                gelu_bf16(i, 0)
-                stage2(i, 2)
-            if i >= 0:
-                weigh(nxt, 2)
-            stage1(nxt, 6)
-            if i >= 0:
-                weigh(nxt, 3)
-            stage1(nxt, 7)
-            if live(far):
-                group_xw(far)
-            if live(i):
-                gelu(i, 1)
-                stage2(i, 3)
-                turn_y(i, 0)
-            weigh(nxt, 4)
-            weigh(nxt, 5)
-            if live(i):
-                gelu(i, 2)
-                gelu(i, 3)
-                store_y(i, slice(0, 4))
-                turn_y(i, 1)
-            weigh(nxt, 6)
-            weigh(nxt, 7)
-            if live(i):
-                group_planes(i, 0, "act")
-            if live(i + 3):
-                scale_rows_act(i + 3)
-            if live(i):
-                group_planes(i, 1, "act")
-
-        prev, last = C - 2, C - 1
-        quantize("xh", last, work)
+        for jh in range(2):
+            turn_x(0, jh)
+            group_xw(0, jh)
+        group_weight("f0", on_vector)
+        group_weight("f1", on_scalar)
+        quantize_x("xw", 0)
+        turn_r()
+        warm_on_zeros(WARM_BETWEEN)
+        quantize_weight("f0")
+        quantize_x("xh", 0)
+        group_r()
+        to_modes(0, 2)
+        for th in range(2):
+            to_modes_wide(0, th)
+            weigh_wide(0, th)
+        scale_rows(1, range(PACK - 1))
+        weigh(0, 2)
+        quantize_weight("f1")
+        scale_rows(1, [PACK - 1])
+        group_xh(1)
+        to_modes(0, 3)
+        group_weight("g0", on_scalar)
+        weigh(0, 3)
+        for jh in range(2):
+            turn_x(1, jh)
+            group_xw(1, jh)
+        group_wide(0)
+        group_weight("g1", on_scalar)
         for k in range(4, 8):
-            stage1(last, k)
-        quantize("vw", prev, work)
-        quantize("vh", prev, work)
-        y_tiles(prev)
-        stage2(prev, 0)
-        stage2(prev, 1)
-        quantize("xw", last, work)
-        planes(prev - 1)
+            to_modes(0, k)
+        keep_warm(0, WARM_AFTER)
+        for k in range(4, 8):
+            weigh(0, k)
+
+        def finish_field(c):
+            to_field(c, 3)
+            turn_y(c, 0)
+            gelu_bf16(c, 3)
+            gelu_f32(c, 3)
+            store_y(c, slice(0, PACK))
+            turn_y(c, 1)
+
+        for c in range(1, C - 1):
+            quantize_x("xw", c)
+            quantize_modes(c - 1)
+            if c == 1:
+                quantize_weight("g0")
+                quantize_weight("g1")
+            quantize_x("xh", c)
+            if c >= 2:
+                finish_field(c - 2)
+                group_out(c - 2, 1, on_scalar)
+                keep_warm(c - 1, WARM_STEP)
+            to_modes_wide(c, 0)
+            if c >= 2:
+                group_out(c - 2, 0, on_scalar)
+            to_modes(c, 2)
+            weigh(c, 2)
+            weigh_wide(c, 0)
+            to_modes_wide(c, 1)
+            to_field(c - 1, 0)
+            if c >= 2:
+                quantize_out(c - 2)
+            scale_rows(c + 1, range(PACK))
+            group_xh(c + 1)
+            weigh_wide(c, 1)
+            to_modes(c, 3)
+            weigh(c, 3)
+            turn_x(c + 1, 1)
+            turn_x(c + 1, 0)
+            to_field(c - 1, 1)
+            group_xw(c + 1, 0)
+            to_modes(c, 4)
+            to_modes(c, 5)
+            gelu_bf16(c - 1, 0)
+            group_xw(c + 1, 1)
+            group_wide(c)
+            weigh(c, 4)
+            gelu_f32(c - 1, 0)
+            to_field(c - 1, 2)
+            weigh(c, 5)
+            to_modes(c, 6)
+            gelu_f32(c - 1, 1)
+            to_modes(c, 7)
+            weigh(c, 6)
+            gelu_bf16(c - 1, 1)
+            weigh(c, 7)
+            gelu_f32(c - 1, 2)
+            gelu_bf16(c - 1, 2)
+
+        last, prev, older = C - 1, C - 2, C - 3
+        quantize_modes(prev)
+        quantize_x("xh", last)
+        finish_field(older)
+        quantize_x("xw", last)
+        group_out(older, 1, on_scalar)
+        keep_warm(prev, WARM_STEP)
+        to_field(prev, 0)
+        to_modes(last, 4)
+        to_modes(last, 5)
+        group_out(older, 0, on_scalar)
+        to_field(prev, 1)
+        quantize_out(older)
+        store_scales(0, prev, (nc.sync, nc.sync))
         weigh(last, 4)
-        stage1(last, 0)
-        gelu(prev, 0)
-        stage2(prev, 2)
+        gelu_f32(prev, 0)
+        gelu_bf16(prev, 0)
+        to_modes(last, 6)
+        gelu_f32(prev, 1)
         weigh(last, 5)
-        stage1(last, 1)
         weigh(last, 6)
-        stage1(last, 2)
-        gelu(prev, 1)
-        stage2(prev, 3)
-        turn_y(prev, 0)
-        weigh(last, 7)
-        stage1(last, 3)
-        weigh(last, 0)
-        quantize("vh", last, work)
-        quantize_block("vw", last, 0)
-        gelu(prev, 2)
-        gelu(prev, 3)
-        store_y(prev, slice(0, 4))
-        y_tiles(last)
-        stage2(last, 0)
-        turn_y(prev, 1)
-        group_planes(prev, 0, "act")
+        gelu_bf16(prev, 1)
+        to_modes(last, 1)
         weigh(last, 1)
+        to_field(prev, 2)
+        to_modes(last, 0)
+        weigh(last, 0)
+        to_modes(last, 7)
+        to_field(prev, 3)
+        to_modes(last, 2)
+        weigh(last, 7)
+        quantize_modes_part(last, block(0))
+        gelu_bf16(prev, 2)
+        to_modes(last, 3)
         weigh(last, 2)
-        quantize_block("vw", last, 1)
-        stage2(last, 1)
-        gelu_f32(last, 0)
-        store_y(last, slice(0, 1))
+        gelu_f32(prev, 2)
+        gelu_bf16(prev, 3)
+        gelu_f32(prev, 3)
+        store_y(prev, slice(0, PACK))
+        turn_y(prev, 0)
+        group_out(prev, 0, on_scalar)
+        quantize_modes_part(last, slice(S, 2 * S))
+        turn_y(prev, 1)
+        group_out(prev, 1, on_scalar)
+        to_field(last, 0)
+        quantize_modes_part(last, block(1))
+        to_field(last, 1)
         weigh(last, 3)
-        quantize_block("vw", last, 2)
-        stage2(last, 2)
-        group_planes(prev, 1, "dve")
-        quantize_block("vw", last, 3)
-        gelu_f32(last, 1)
-        store_y(last, slice(1, 2))
-        stage2(last, 3)
-        round_y(last, 0)
-        round_y(last, 1)
-        turn_y(last, 0)
-        planes(prev)
+        quantize_modes_part(last, block(2))
+        for j in range(2):
+            gelu_f32(last, j)
+            store_y(last, slice(j, j + 1))
+        to_field(last, 2)
         gelu_f32(last, 2)
         store_y(last, slice(2, 3))
+        quantize_modes_part(last, block(3))
+        to_field(last, 3)
         gelu_bf16(last, 3)
-        round_y(last, 2)
-        turn_y(last, 1)
         gelu_f32(last, 3)
         store_y(last, slice(3, 4))
-        group_planes(last, 0, "act")
-        group_planes(last, 1, "dve")
-        planes(last)
+        for j in range(3):
+            round_y(last, j)
+        turn_y(last, 0)
+        quantize_out(prev)
+        group_out(last, 0, on_scalar)
+        turn_y(last, 1)
+        for h in range(2):
+            group_out(last, 1, on_vector, slice(P // 2 * h, P // 2 * (h + 1)))
+        for h in range(2):
+            quantize_out(last, half(h))
+        store_scales(prev, C, (nc.sync, nc.scalar))

@@ -3,459 +3,336 @@ from contextlib import ExitStack
 import concourse.mybir as mybir
 from concourse.masks import make_identity
 
+C, L, P, PACK = 8, 512, 128, 4
+FLOPS = 4 * 2 * C * L * L * L
+
 F32 = mybir.dt.float32
 BF16 = mybir.dt.bfloat16
-I32 = mybir.dt.int32
 U32 = mybir.dt.uint32
+I32 = mybir.dt.int32
 U8 = mybir.dt.uint8
 FP8X4 = mybir.dt.float8_e4m3fn_x4
-MULT = mybir.AluOpType.mult
-GELU = mybir.ActivationFunctionType.Gelu_apprx_tanh
-COPY = mybir.ActivationFunctionType.Copy
+ALU = mybir.AluOpType
+ACT = mybir.ActivationFunctionType
 
-C = 8
-S = 512
-P = 128
-PACK = 4
-HALF = S // 2
-ALIGN = 64
-FLOPS = 4 * 2 * C * S * S * S
-
-TURN_BANKS, MODE_BANKS, FIELD_BANKS = 2, 4, 2
-
-WARM_BEFORE, WARM_BETWEEN, WARM_AFTER, WARM_STEP = 12, 10, 5, 2
-
-
-def block(b):
-    return slice(P * b, P * (b + 1))
-
-
-def half(h):
-    return slice(HALF * h, HALF * (h + 1))
-
-
-def by_slots(rows):
-    return rows.rearrange("(p j) n -> p j n", j=PACK)
-
-
-def flat(grouped_tile):
-    return grouped_tile.rearrange("p n t -> p (n t)")
+A_ROW = 0
+R_ROW = 2
+N_ROWS = 2 + 2 * C
+GROUP = 4
 
 
 def tile_factorizedtwoaxisspectraloperator_x1_kernel(tc, x, a, f, r, g, out_0, out_1, out_2):
     nc = tc.nc
-    words_out = out_1[0].rearrange("p m t -> p (m t)").bitcast(I32)
-    scales_out = out_2[0].bitcast(I32)
-
     with ExitStack() as ctx:
-        keep = ctx.enter_context(tc.tile_pool(name="keep", bufs=1))
-        work = ctx.enter_context(tc.tile_pool(name="work", bufs=2))
-        psum = ctx.enter_context(tc.psum_pool(name="psum", bufs=2))
+        sb = ctx.enter_context(tc.tile_pool(name="sb", bufs=1))
+        ps = ctx.enter_context(tc.psum_pool(name="ps", bufs=1))
         ctx.enter_context(tc.manual_schedule())
 
-        ident = keep.tile([P, P], F32, name="ident", align_bytes=ALIGN)
-        make_identity(nc, ident[:])
+        def tiles(name, count, shape, dtype):
+            return [sb.tile(shape, dtype, name="%s%d" % (name, i), align_bytes=64) for i in range(count)]
 
-        a_sb = keep.tile([P, 2, PACK], BF16, name="a_sb", align_bytes=ALIGN)
-        r_rows = keep.tile([P, S], BF16, name="r_rows", align_bytes=ALIGN)
-        r_sb = keep.tile([P, 2 * C, PACK], BF16, name="r_sb", align_bytes=ALIGN)
-        r0_f32 = keep.tile([P, C, PACK], F32, name="r0_f32", align_bytes=ALIGN)
-        x_sb = [keep.tile([P, PACK, S], BF16, name="x_sb%d" % c, align_bytes=ALIGN) for c in range(C)]
-        w_hbm = {"f0": f[0], "f1": f[1], "g0": g[0], "g1": g[1]}
-        w_sb = {w: keep.tile([P, PACK, S], BF16, name="raw_" + w, align_bytes=ALIGN) for w in w_hbm}
-        out_scales = keep.tile([P, C * S], U8, name="out_scales", align_bytes=ALIGN)
-        idle_codes = keep.tile([P, P], U32, name="idle_codes", align_bytes=ALIGN)
-        idle_scales = keep.tile([P, P], U8, name="idle_scales", align_bytes=ALIGN)
-        table_warm = keep.tile([P, 1], F32, name="table_warm")
+        def quantised(name, count):
+            return list(zip(tiles(name + "_codes", count, [P, L], U32), tiles(name + "_scales", count, [P, L], U8)))
 
-        nc.scalar.dma_start(out=a_sb[:], in_=a.rearrange("q (p t) -> p q t", t=PACK))
-        nc.vector.memset(r_rows[:], 0.0)
-        nc.vector.quantize_mx(out=idle_codes[:].bitcast(FP8X4), scales=idle_scales[:], in_=r_rows[:])
-        nc.scalar.activation(out=table_warm[:], in_=ident[:, 0:1], func=GELU)
+        vector_banks = [ps.tile([P, L], F32, name="vbank%d" % i) for i in range(4)]
+        scalar_banks = [ps.tile([P, L], F32, name="sbank%d" % i) for i in range(4)]
 
-        for jh in range(2):
-            slots = slice(2 * jh, 2 * jh + 2)
-            nc.sync.dma_start(out=x_sb[0][:, slots, :], in_=by_slots(x[0])[:, slots, :])
-        nc.sync.dma_start(out=w_sb["f0"][:], in_=by_slots(w_hbm["f0"]))
-        nc.sync.dma_start(out=r_rows[0 : 2 * C, :], in_=r.rearrange("q c m -> (q c) m"))
-        for dst, src in (
-            [(w_sb["f1"], w_hbm["f1"]), (x_sb[1], x[1])]
-            + [(w_sb["g0"], w_hbm["g0"]), (x_sb[2], x[2]), (w_sb["g1"], w_hbm["g1"])]
-            + [(x_sb[c], x[c]) for c in range(3, C)]
-        ):
-            nc.sync.dma_start(out=dst[:], in_=by_slots(src))
+        def vbank(c, use):
+            return vector_banks[(6 * c + use) % 4]
 
-        grouped, codes, scales, banks, staged = {}, {}, {}, {}, {}
+        def sbank(c, use):
+            return scalar_banks[(10 * c + use) % 4]
 
-        def stage_tile(name, c, shape, dtype, bufs=2):
-            if (name, c) not in staged:
-                staged[name, c] = work.tile(shape, dtype, name=name, align_bytes=ALIGN, bufs=bufs)
-            return staged[name, c]
+        ident = sb.tile([P, P], F32, name="ident", align_bytes=64)
+        rows = sb.tile([P, L], BF16, name="rows", align_bytes=64)
+        fac32 = sb.tile([P, N_ROWS, PACK], F32, name="fac32", align_bytes=64)
+        warm = sb.tile([P, 16], F32, name="warm", align_bytes=64)
+        a0 = sb.tile([P, PACK], BF16, name="a0", align_bytes=64)
+        x_h = tiles("x_h", C, [P, PACK, L], BF16)
+        x_w = tiles("x_w", C, [P, PACK, L], BF16)
+        w_raw = tiles("w_raw", 4, [P, PACK, L], BF16)
+        w_words = tiles("w_words", 4, [P, L, PACK], BF16)
+        w_q = quantised("w", 4)
+        F0, F1, G0, G1 = range(4)
+        xh_rows = tiles("xh_rows", 1, [P, PACK, L], BF16)
+        xh = tiles("xh", 1, [P, L, PACK], BF16)
+        xw = tiles("xw", 1, [P, L, PACK], BF16)
+        vw_rows = tiles("vw_rows", 2, [P, PACK, L], BF16)
+        vw = tiles("vw", 1, [P, L, PACK], BF16)
+        vh = tiles("vh", 1, [P, L, PACK], BF16)
+        xh_q, xw_q, vh_q, vw_q = (quantised(n, 2) for n in ("xh", "xw", "vh", "vw"))
+        y = tiles("y", 3 * PACK, [P, L], F32)
+        y16 = tiles("y16", 2 * PACK, [P, 2, P, 2], BF16)
+        yt = tiles("yt", 2, [P, L, PACK], BF16)
+        y_codes = tiles("y_codes", 2, [P, L], U32)
+        y_scales = tiles("y_scales", C // GROUP, [P, L], U8)
 
-        def modes_tile(c):
-            return stage_tile("grouped_v", c, [P, 2 * S, PACK], BF16)
+        def quantise(dst, words):
+            codes, scales = dst
+            nc.vector.quantize_mx(out=codes.bitcast(FP8X4), scales=scales, in_=words.rearrange("p n t -> p (n t)"))
 
-        def field_bank(c, j):
-            if ("y", c, j) not in banks:
-                if c == C - 1 and j % 2:
-                    banks["y", c, j] = psum.tile([P, S], F32, name="modes", bufs=MODE_BANKS)
-                else:
-                    banks["y", c, j] = psum.tile([P, S], F32, name="field", bufs=FIELD_BANKS)
-            return banks["y", c, j]
+        def whole(pair):
+            return pair[0][:], pair[1][:]
 
-        def interleave_on_scalar(dst, src):
-            nc.scalar.copy(out=dst.rearrange("p (n i) t -> p n t i", i=4), in_=src.rearrange("p t (n i) -> p n t i", i=4))
-
-        def quantize_into(name, grouped_ap, pool):
-            width = grouped_ap.shape[1]
-            tag = name[0]
-            codes[name] = pool.tile([P, width], U32, name="codes_" + tag, align_bytes=ALIGN)
-            scales[name] = pool.tile([P, width], U8, name="scales_" + tag, align_bytes=ALIGN)
-            nc.vector.quantize_mx(out=codes[name][:].bitcast(FP8X4), scales=scales[name][:], in_=flat(grouped_ap))
-
-        def mx(out, lhs, lhs_cols, rhs, rhs_cols, start=True, stop=True):
+        def mx(out, lhs, lhs_cols, rhs, rhs_cols, start, stop):
             nc.tensor.matmul_mx(
                 out=out,
-                lhsT=codes[lhs][:, lhs_cols].bitcast(FP8X4),
-                lhsT_scale=scales[lhs][:, lhs_cols],
-                rhs=codes[rhs][:, rhs_cols].bitcast(FP8X4),
-                rhs_scale=scales[rhs][:, rhs_cols],
+                lhsT=lhs[0][:, lhs_cols].bitcast(FP8X4),
+                lhsT_scale=lhs[1][:, lhs_cols],
+                rhs=rhs[0][:, rhs_cols].bitcast(FP8X4),
+                rhs_scale=rhs[1][:, rhs_cols],
                 start=start,
                 stop=stop,
             )
 
+        def block(i):
+            return slice(P * i, P * (i + 1))
 
-        def group_weight(w, copy):
-            grouped[w] = work.tile([P, S, PACK], BF16, name="grouped_weight", align_bytes=ALIGN)
-            if w == "g0":
-                interleave_on_scalar(grouped[w][:], w_sb[w][:])
-            else:
+        ALL = slice(0, L)
+
+        def interleave_views(words, slots):
+            return (
+                words.rearrange("p (c i) t -> p c t i", i=4),
+                slots.rearrange("p t (c i) -> p c t i", i=4),
+            )
+
+        def load_weight(i, src):
+            nc.sync.dma_start(out=w_raw[i][:], in_=src.rearrange("(p t) n -> p t n", t=PACK))
+
+        def load_x_h(c):
+            nc.sync.dma_start(out=x_h[c][:], in_=x[c].rearrange("(p t) w -> p t w", t=PACK))
+
+        def load_x_w(c):
+            nc.sync.dma_start(out=x_w[c][:], in_=x[c].rearrange("(j p) w -> p j w", p=P))
+
+        def weight_words(i, copy):
+            if i in (F0, F1):
                 copy(
-                    out=grouped[w][:].rearrange("p (t i) j -> p t i j", t=PACK),
-                    in_=w_sb[w][:].rearrange("p j (i t) -> p t i j", t=PACK),
+                    out=w_words[i][:].rearrange("p (s m) t -> p m t s", s=PACK),
+                    in_=w_raw[i][:].rearrange("p t (m s) -> p m t s", s=PACK),
                 )
-
-        def quantize_weight(w):
-            quantize_into((w,), grouped[w][:], keep)
-
-        def turn_r():
-            banks["r"] = psum.tile([P, 2, P], F32, name="turn", bufs=TURN_BANKS)
-            for u in range(2):
-                nc.tensor.transpose(banks["r"][:, u, :], r_rows[:].bitcast(F32)[:, u : 2 * P : 2], ident[:])
-
-        def group_r():
-            nc.vector.tensor_copy(out=r_sb[:].bitcast(F32), in_=banks["r"][:, :, 0 : 2 * C].rearrange("p u n -> p n u"))
-            nc.scalar.copy(out=r0_f32[:], in_=r_sb[:, 0:C, :])
-
-        def warm_on_zeros(passes):
-            codes["idle",], scales["idle",] = idle_codes, idle_scales
-            for k in range(passes):
-                mx(field_bank(0, 0)[:, block(k % PACK)], ("idle",), block(0), ("idle",), block(0))
-
-        def keep_warm(c, passes):
-            for k in range(passes):
-                mx(field_bank(c, 0)[:], ("f0",), block(0), ("f1",), slice(0, S))
-
-
-        def scale_rows(c, slots):
-            scaled = stage_tile("scaled", c, [P, PACK, S], BF16)
-            for j in slots:
-                nc.vector.tensor_scalar(
-                    out=scaled[:, j, :], in0=x_sb[c][:, j, :], scalar1=a_sb[:, 1, j : j + 1], scalar2=None, op0=MULT
-                )
-
-        def group_xh(c):
-            dst = stage_tile("grouped_xh", c, [P, S, PACK], BF16, bufs=1)
-            scaled = staged["scaled", c]
-            if c == 0:
-                interleave_on_scalar(dst[:], scaled[:])
             else:
-                nc.gpsimd.tensor_scalar(
-                    out=dst[:], in0=scaled[:].rearrange("p t n -> p n t"), scalar1=1.0, scalar2=1.0, op0=MULT, op1=MULT
-                )
+                dst, src = interleave_views(w_words[i][:], w_raw[i][:])
+                copy(out=dst, in_=src)
 
-        def turn_x(c, jh):
-            words = x_sb[c][:].bitcast(F32)
-            bank = psum.tile([P, 2, 2, P], F32, name="turn", bufs=TURN_BANKS)
-            banks["xw", c, jh] = bank
-            for u in range(2):
-                for jj in range(2):
-                    nc.tensor.transpose(bank[:, u, jj, :], words[:, 2 * jh + jj, u : 2 * P : 2], ident[:])
-
-        def group_xw(c, jh):
-            dst = stage_tile("grouped_xw", c, [P, S, PACK], BF16)
-            src = banks["xw", c, jh][:].rearrange("p u j i -> p (u j i)").bitcast(BF16)
-            factor = a_sb[:, 0, :].rearrange("p (u e) -> p u e", e=2).unsqueeze(1).to_broadcast([P, HALF, 2, 2])
-            nc.vector.tensor_tensor(
-                out=dst[:, half(jh), :].rearrange("p n (u e) -> p n u e", e=2),
-                in0=src.rearrange("p (u n e) -> p n u e", u=2, e=2),
-                in1=factor,
-                op=MULT,
-            )
-
-        def quantize_x(kind, c):
-            quantize_into((kind, c), staged["grouped_" + kind, c][:], work)
-
-        def to_modes(c, k):
-            q, b = divmod(k, PACK)
-            bank = psum.tile([P, PACK, P], F32, name="modes", bufs=MODE_BANKS)
-            banks["u", c, k] = bank
+        def scale_xh(c):
             for t in range(PACK):
-                mx(bank[:, t, :], (("f0", "f1")[q],), block(t), (("xw", "xh")[q], c), block(b))
-
-        def weigh(c, k):
-            factor = r_sb[:, C * (k // PACK) + c, :].unsqueeze(1).to_broadcast([P, P, PACK])
-            nc.vector.tensor_tensor(
-                out=modes_tile(c)[:, block(k), :], in0=banks["u", c, k][:].rearrange("p t n -> p n t"), in1=factor, op=MULT
-            )
-
-        def to_modes_wide(c, th):
-            bank = psum.tile([P, 2, HALF], F32, name="modes", bufs=MODE_BANKS)
-            banks["wide", c, th] = bank
-            for tt in range(2):
-                mx(bank[:, tt, :], ("f0",), block(2 * th + tt), ("xw", c), half(0))
-
-        def weigh_wide(c, th):
-            weighed = stage_tile("weighed", c, [P, PACK, HALF], BF16)
-            for tt in range(2):
-                t = 2 * th + tt
-                nc.scalar.activation(
-                    out=weighed[:, t, :], in_=banks["wide", c, th][:, tt, :], func=COPY, scale=r0_f32[:, c, t : t + 1]
+                nc.vector.tensor_scalar(
+                    out=xh_rows[0][:, t, :], in0=x_h[c][:, t, :], scalar1=fac32[:, A_ROW + 1, t : t + 1], scalar2=None, op0=ALU.mult
                 )
 
-        def group_wide(c):
-            interleave_on_scalar(modes_tile(c)[:, half(0), :], staged["weighed", c][:])
+        def interleave_xh(c):
+            if c == 0:
+                dst, src = interleave_views(xh[0][:], xh_rows[0][:])
+                nc.vector.tensor_copy(out=dst, in_=src)
+            else:
+                src = xh_rows[0][:].rearrange("p t n -> p n t")
+                nc.gpsimd.tensor_scalar(out=xh[0][:], in0=src, scalar1=1.0, scalar2=0.0, op0=ALU.mult, op1=ALU.add)
 
-        def quantize_modes(c):
-            quantize_into(("v", c), modes_tile(c)[:], work)
-
-        def quantize_modes_part(c, cols):
-            if ("v", c) not in codes:
-                codes["v", c] = work.tile([P, 2 * S], U32, name="codes_v", align_bytes=ALIGN)
-                scales["v", c] = work.tile([P, 2 * S], U8, name="scales_v", align_bytes=ALIGN)
-            nc.vector.quantize_mx(
-                out=codes["v", c][:, cols].bitcast(FP8X4), scales=scales["v", c][:, cols], in_=flat(modes_tile(c)[:, cols, :])
-            )
-
-        def to_field(c, j):
-            bank = field_bank(c, j)
-            mx(bank[:], ("v", c), block(j), ("g0",), slice(0, S), stop=False)
-            mx(bank[:], ("g1",), block(j), ("v", c), slice(S, 2 * S), start=False)
-
-        def by_words(row):
-            return row.rearrange("p (i u e) -> p u i e", u=2, e=2)
-
-        def y_f32(c):
-            return stage_tile("y_f32", c, [P, PACK, S], F32)
-
-        def y_bf16_slot(c, j):
-            return stage_tile("y_bf16", c, [P, PACK, S], BF16)[:, j, :].rearrange("p (u i e) -> p u i e", u=2, e=2)
-
-        def gelu_f32(c, j):
-            nc.scalar.activation(out=y_f32(c)[:, j, :], in_=banks["y", c, j][:], func=GELU)
-
-        def gelu_bf16(c, j):
-            nc.scalar.activation(out=y_bf16_slot(c, j), in_=by_words(banks["y", c, j][:]), func=GELU)
-
-        def round_y(c, j):
-            nc.vector.tensor_copy(out=y_bf16_slot(c, j), in_=by_words(y_f32(c)[:, j, :]))
-
-        def store_y(c, slots):
-            nc.sync.dma_start(out=by_slots(out_0[c])[:, slots, :], in_=y_f32(c)[:, slots, :])
-
-        def turn_y(c, jh):
-            words = staged["y_bf16", c][:].bitcast(F32)
-            bank = psum.tile([P, 2, 2, P], F32, name="turn", bufs=TURN_BANKS)
-            banks["out", c, jh] = bank
-            for jj in range(2):
+        def transpose_x(c):
+            words = x_w[c][:].bitcast(F32)
+            for half in range(2):
+                bank = vbank(c - 1, half)
                 for u in range(2):
-                    nc.tensor.transpose(bank[:, jj, u, :], words[:, 2 * jh + jj, block(u)], ident[:])
+                    for j in range(2):
+                        nc.tensor.transpose(bank[:, block(2 * u + j)], words[:, 2 * half + j, u::2], ident[:])
 
-        def group_out(c, jh, copy, rows=slice(0, P)):
-            words = flat(stage_tile("grouped_out", c, [P, S, PACK], BF16)[:]).bitcast(F32)
+        def scale_xw(c, half):
+            bank = vbank(c - 1, half)
+            nc.vector.tensor_tensor(
+                out=xw[0][:, 256 * half : 256 * (half + 1), :].rearrange("p n (u e) -> p n u e", e=2),
+                in0=bank[:].bitcast(BF16).rearrange("p (u n e) -> p n u e", u=2, e=2),
+                in1=a0[:].rearrange("p (u e) -> p u e", e=2).unsqueeze(1).to_broadcast([P, 256, 2, 2]),
+                op=ALU.mult,
+            )
+
+        def modes_h(c, s):
+            bank = vbank(c, 2 + s)
+            for t in range(PACK):
+                mx(bank[:, block(t)], w_q[F1], block(t), xh_q[c % 2], block(s), True, True)
+
+        def scale_vh(c, s):
+            bank = vbank(c, 2 + s)
+            nc.vector.tensor_tensor(
+                out=vh[0][:, block(s), :],
+                in0=bank[:].rearrange("p (t n) -> p n t", t=PACK),
+                in1=fac32[:, R_ROW + C + c, :].unsqueeze(1).to_broadcast([P, P, PACK]),
+                op=ALU.mult,
+            )
+
+        def modes_w(c, t):
+            bank = sbank(c - 1, 2 + t)
+            mx(bank[:], w_q[F0], block(t), xw_q[c % 2], ALL, True, True)
+            nc.scalar.activation(out=vw_rows[c % 2][:, t, :], in_=bank[:], func=ACT.Copy, scale=fac32[:, R_ROW + c, t : t + 1])
+
+        def interleave_vw(c, cols):
+            dst, src = interleave_views(vw[0][:, cols, :], vw_rows[c % 2][:, :, cols])
+            nc.vector.tensor_copy(out=dst, in_=src)
+
+        def quantise_vw(c, cols):
+            codes, scales = vw_q[c % 2]
+            quantise((codes[:, cols], scales[:, cols]), vw[0][:, cols, :])
+
+        def result(c, j, bank):
+            mx(bank[:], vw_q[c % 2], block(j), w_q[G0], ALL, True, False)
+            mx(bank[:], w_q[G1], block(j), vh_q[c % 2], ALL, False, True)
+            tile = y[PACK * (c % 3) + j]
+            nc.scalar.activation(out=tile[:], in_=bank[:], func=ACT.Gelu_apprx_tanh)
+            nc.sync.dma_start(out=out_0[c, block(j), :], in_=tile[:])
+
+        def round_y(c, j, copy):
             copy(
-                out=words.rearrange("p (i k) -> p i k", k=8)[:, rows, 4 * jh : 4 * jh + 4],
-                in_=banks["out", c, jh][:].rearrange("p j u i -> p i (j u)")[:, rows, :],
+                out=y16[PACK * (c % 2) + j][:],
+                in_=y[PACK * (c % 3) + j][:].rearrange("p (q u e) -> p u q e", u=2, e=2),
             )
 
-        def quantize_out(c, cols=slice(0, S)):
-            out_codes = work.tile([P, cols.stop - cols.start], U32, name="out_codes", align_bytes=ALIGN, bufs=3)
-            at = slice(S * c + cols.start, S * c + cols.stop)
-            nc.vector.quantize_mx(
-                out=out_codes[:].bitcast(FP8X4), scales=out_scales[:, at], in_=flat(staged["grouped_out", c][:, cols, :])
-            )
-            nc.sync.dma_start(out=words_out[:, at], in_=out_codes[:].bitcast(I32))
+        def transpose_y(c, js, bank):
+            for u in range(2):
+                for i, j in enumerate(js):
+                    words = y16[PACK * (c % 2) + j][:].rearrange("p u q e -> p (u q e)").bitcast(F32)
+                    nc.tensor.transpose(bank[:, block(len(js) * u + i)], words[:, block(u)], ident[:])
 
-        def store_scales(first, stop, queues):
+        def collect_y(c, js, bank, copy):
+            n = P * len(js)
+            words = yt[c % 2][:].rearrange("p n t -> p (n t)").bitcast(F32)
+            copy(
+                out=words[:, 2 * P * js[0] : 2 * P * js[0] + 2 * n].rearrange("p (n u) -> p n u", u=2),
+                in_=bank[:, 0 : 2 * n].rearrange("p (u n) -> p n u", u=2),
+            )
+
+        words_out = out_1.rearrange("g p m t -> p (g m t)").bitcast(I32)
+        scales_out = out_2.rearrange("g q m -> q (g m)").bitcast(I32)
+
+        def quantise_y(c, cols):
+            quantise((y_codes[c % 2][:, cols], y_scales[c // GROUP][4 * (c % GROUP) :, cols]), yt[c % 2][:, cols, :])
+
+        def store_words(c, cols):
+            codes = y_codes[c % 2]
+            nc.sync.dma_start(out=words_out[:, L * c + cols.start : L * c + cols.stop], in_=codes[:, cols].bitcast(I32))
+
+        def planes(c, cols):
+            quantise_y(c, cols)
+            store_words(c, cols)
+
+        def store_scales(group, queues):
+            first = group * GROUP * (L // 4)
             for quad in range(4):
-                queues[quad % 2].dma_start(
-                    out=scales_out[4 * quad : 4 * quad + 4, P * first : P * stop],
-                    in_=out_scales[32 * quad : 32 * quad + 4, S * first : S * stop].bitcast(I32),
+                queues[quad % len(queues)].dma_start(
+                    out=scales_out[4 * quad : 4 * quad + 4, first : first + GROUP * (L // 4)].rearrange("q (k n) -> k q n", k=GROUP),
+                    in_=y_scales[group][32 * quad : 32 * quad + 16, :].bitcast(I32),
                 )
 
-        on_scalar, on_vector = nc.scalar.copy, nc.vector.tensor_copy
+        nc.vector.memset(rows[:], 0.0)
+        nc.scalar.dma_start(out=rows[A_ROW:R_ROW, :], in_=a)
+        nc.scalar.dma_start(out=rows[R_ROW:N_ROWS, :], in_=r.rearrange("q c m -> (q c) m"))
+        nc.vector.memset(warm[:, 0:1], 0.0)
+        nc.scalar.activation(out=warm[:, 8:9], in_=warm[:, 0:1], func=ACT.Gelu_apprx_tanh)
+        make_identity(nc, ident[:])
+        load_weight(F1, f[1])
+        load_x_h(0)
+        load_weight(F0, f[0])
+        load_x_w(0)
+        load_x_w(1)
+        load_x_h(1)
+        load_weight(G0, g[0])
+        load_weight(G1, g[1])
+        for c in range(2, C):
+            load_x_h(c)
+            load_x_w(c)
 
-        warm_on_zeros(WARM_BEFORE)
-        scale_rows(0, range(PACK))
-        group_xh(0)
-        for jh in range(2):
-            turn_x(0, jh)
-            group_xw(0, jh)
-        group_weight("f0", on_vector)
-        group_weight("f1", on_scalar)
-        quantize_x("xw", 0)
-        turn_r()
-        warm_on_zeros(WARM_BETWEEN)
-        quantize_weight("f0")
-        quantize_x("xh", 0)
-        group_r()
-        to_modes(0, 2)
-        for th in range(2):
-            to_modes_wide(0, th)
-            weigh_wide(0, th)
-        scale_rows(1, range(PACK - 1))
-        weigh(0, 2)
-        quantize_weight("f1")
-        scale_rows(1, [PACK - 1])
-        group_xh(1)
-        to_modes(0, 3)
-        group_weight("g0", on_scalar)
-        weigh(0, 3)
-        for jh in range(2):
-            turn_x(1, jh)
-            group_xw(1, jh)
-        group_wide(0)
-        group_weight("g1", on_scalar)
-        for k in range(4, 8):
-            to_modes(0, k)
-        keep_warm(0, WARM_AFTER)
-        for k in range(4, 8):
-            weigh(0, k)
+        bank = scalar_banks[0]
+        row_words = rows[:].bitcast(F32)
+        for u in range(2):
+            nc.tensor.transpose(bank[:, block(u)], row_words[:, u::2], ident[:])
+        turned = bank[:, 0 : 2 * P].bitcast(BF16).rearrange("p (u n e) -> p n u e", u=2, e=2)
+        weight_words(F1, nc.vector.tensor_copy)
+        nc.vector.tensor_copy(out=fac32[:].rearrange("p n (u e) -> p n u e", e=2), in_=turned[:, 0:N_ROWS])
+        nc.vector.tensor_copy(out=a0[:].rearrange("p (u e) -> p u e", e=2), in_=turned[:, A_ROW])
+        quantise(whole(w_q[F1]), w_words[F1][:])
+        weight_words(F0, nc.scalar.copy)
+        scale_xh(0)
+        transpose_x(0)
+        interleave_xh(0)
+        scale_xw(0, 0)
+        scale_xw(0, 1)
+        transpose_x(1)
+        quantise(whole(xh_q[0]), xh[0][:])
+        quantise(whole(w_q[F0]), w_words[F0][:])
+        quantise(whole(xw_q[0]), xw[0][:])
+        modes_h(0, 0)
+        modes_h(0, 1)
+        for t in range(PACK):
+            modes_w(0, t)
+        weight_words(G0, nc.scalar.copy)
+        weight_words(G1, nc.scalar.copy)
+        scale_xh(1)
 
-        def finish_field(c):
-            to_field(c, 3)
-            turn_y(c, 0)
-            gelu_bf16(c, 3)
-            gelu_f32(c, 3)
-            store_y(c, slice(0, PACK))
-            turn_y(c, 1)
+        HALVES = ((0, 1), (2, 3))
+        last = C - 1
+        for c in range(last):
+            interleave_xh(c + 1)
+            for half in range(2):
+                scale_xw(c + 1, half)
+                modes_h(c, 2 + half)
+            for s in range(PACK):
+                scale_vh(c, s)
+            if c + 2 < C:
+                transpose_x(c + 2)
+            if c >= 1:
+                for j in range(PACK):
+                    round_y(c - 1, j, nc.scalar.copy)
+                for half in range(2):
+                    transpose_y(c - 1, HALVES[half], sbank(c, half))
+                for half in range(2):
+                    collect_y(c - 1, HALVES[half], sbank(c, half), nc.scalar.copy)
+            quantise(whole(xh_q[(c + 1) % 2]), xh[0][:])
+            quantise(whole(xw_q[(c + 1) % 2]), xw[0][:])
+            for s in range(2 if c + 2 < C else PACK):
+                modes_h(c + 1, s)
+            for t in range(PACK):
+                modes_w(c + 1, t)
+            interleave_vw(c, ALL)
+            quantise(whole(vh_q[c % 2]), vh[0][:])
+            quantise_vw(c, ALL)
+            if c == 0:
+                quantise(whole(w_q[G0]), w_words[G0][:])
+                quantise(whole(w_q[G1]), w_words[G1][:])
+            for j in range(PACK):
+                result(c, j, sbank(c, 6 + j))
+            if c + 2 < C:
+                if c >= 1:
+                    planes(c - 1, ALL)
+                scale_xh(c + 2)
+            if c == GROUP:
+                store_scales(0, [nc.sync])
 
-        for c in range(1, C - 1):
-            quantize_x("xw", c)
-            quantize_modes(c - 1)
-            if c == 1:
-                quantize_weight("g0")
-                quantize_weight("g1")
-            quantize_x("xh", c)
-            if c >= 2:
-                finish_field(c - 2)
-                group_out(c - 2, 1, on_scalar)
-                keep_warm(c - 1, WARM_STEP)
-            to_modes_wide(c, 0)
-            if c >= 2:
-                group_out(c - 2, 0, on_scalar)
-            to_modes(c, 2)
-            weigh(c, 2)
-            weigh_wide(c, 0)
-            to_modes_wide(c, 1)
-            to_field(c - 1, 0)
-            if c >= 2:
-                quantize_out(c - 2)
-            scale_rows(c + 1, range(PACK))
-            group_xh(c + 1)
-            weigh_wide(c, 1)
-            to_modes(c, 3)
-            weigh(c, 3)
-            turn_x(c + 1, 1)
-            turn_x(c + 1, 0)
-            to_field(c - 1, 1)
-            group_xw(c + 1, 0)
-            to_modes(c, 4)
-            to_modes(c, 5)
-            gelu_bf16(c - 1, 0)
-            group_xw(c + 1, 1)
-            group_wide(c)
-            weigh(c, 4)
-            gelu_f32(c - 1, 0)
-            to_field(c - 1, 2)
-            weigh(c, 5)
-            to_modes(c, 6)
-            gelu_f32(c - 1, 1)
-            to_modes(c, 7)
-            weigh(c, 6)
-            gelu_bf16(c - 1, 1)
-            weigh(c, 7)
-            gelu_f32(c - 1, 2)
-            gelu_bf16(c - 1, 2)
-
-        last, prev, older = C - 1, C - 2, C - 3
-        quantize_modes(prev)
-        quantize_x("xh", last)
-        finish_field(older)
-        quantize_x("xw", last)
-        group_out(older, 1, on_scalar)
-        keep_warm(prev, WARM_STEP)
-        to_field(prev, 0)
-        to_modes(last, 4)
-        to_modes(last, 5)
-        group_out(older, 0, on_scalar)
-        to_field(prev, 1)
-        quantize_out(older)
-        store_scales(0, prev, (nc.sync, nc.sync))
-        weigh(last, 4)
-        gelu_f32(prev, 0)
-        gelu_bf16(prev, 0)
-        to_modes(last, 6)
-        gelu_f32(prev, 1)
-        weigh(last, 5)
-        weigh(last, 6)
-        gelu_bf16(prev, 1)
-        to_modes(last, 1)
-        weigh(last, 1)
-        to_field(prev, 2)
-        to_modes(last, 0)
-        weigh(last, 0)
-        to_modes(last, 7)
-        to_field(prev, 3)
-        to_modes(last, 2)
-        weigh(last, 7)
-        quantize_modes_part(last, block(0))
-        gelu_bf16(prev, 2)
-        to_modes(last, 3)
-        weigh(last, 2)
-        gelu_f32(prev, 2)
-        gelu_bf16(prev, 3)
-        gelu_f32(prev, 3)
-        store_y(prev, slice(0, PACK))
-        turn_y(prev, 0)
-        group_out(prev, 0, on_scalar)
-        quantize_modes_part(last, slice(S, 2 * S))
-        turn_y(prev, 1)
-        group_out(prev, 1, on_scalar)
-        to_field(last, 0)
-        quantize_modes_part(last, block(1))
-        to_field(last, 1)
-        weigh(last, 3)
-        quantize_modes_part(last, block(2))
-        for j in range(2):
-            gelu_f32(last, j)
-            store_y(last, slice(j, j + 1))
-        to_field(last, 2)
-        gelu_f32(last, 2)
-        store_y(last, slice(2, 3))
-        quantize_modes_part(last, block(3))
-        to_field(last, 3)
-        gelu_bf16(last, 3)
-        gelu_f32(last, 3)
-        store_y(last, slice(3, 4))
-        for j in range(3):
-            round_y(last, j)
-        turn_y(last, 0)
-        quantize_out(prev)
-        group_out(last, 0, on_scalar)
-        turn_y(last, 1)
-        for h in range(2):
-            group_out(last, 1, on_vector, slice(P // 2 * h, P // 2 * (h + 1)))
-        for h in range(2):
-            quantize_out(last, half(h))
-        store_scales(prev, C, (nc.sync, nc.scalar))
+        lower, upper = slice(0, L // 2), slice(L // 2, L)
+        for s in range(PACK):
+            scale_vh(last, s)
+        interleave_vw(last, lower)
+        quantise(whole(vh_q[last % 2]), vh[0][:])
+        quantise_vw(last, lower)
+        interleave_vw(last, upper)
+        planes(last - 2, ALL)
+        quantise_vw(last, upper)
+        round_y(last - 1, 0, nc.scalar.copy)
+        for j in range(1, PACK):
+            round_y(last - 1, j, nc.vector.tensor_copy)
+        for j in range(PACK):
+            result(last, j, vector_banks[j])
+        for half in range(2):
+            transpose_y(last - 1, HALVES[half], scalar_banks[half])
+        round_y(last, 0, nc.vector.tensor_copy)
+        round_y(last, 1, nc.vector.tensor_copy)
+        collect_y(last - 1, HALVES[0], scalar_banks[0], nc.vector.tensor_copy)
+        collect_y(last - 1, HALVES[1], scalar_banks[1], nc.scalar.copy)
+        round_y(last, 2, nc.vector.tensor_copy)
+        round_y(last, 3, nc.vector.tensor_copy)
+        planes(last - 1, ALL)
+        for j in range(PACK):
+            transpose_y(last, (j,), vector_banks[j])
+            collect_y(last, (j,), vector_banks[j], nc.scalar.copy)
+            quantise_y(last, block(j))
+            if j % 2 == 1:
+                store_words(last, (lower, upper)[j // 2])
+        store_scales(1, [nc.scalar, nc.sync])

@@ -19,6 +19,9 @@ A_ROW = 0
 R_ROW = 2
 N_ROWS = 2 + 2 * C
 GROUP = 4
+W_USE = (0, 2, 4, 5)
+T_USE = (1, 3)
+R_USE = 6
 
 
 def tile_factorizedtwoaxisspectraloperator_x1_kernel(tc, x, a, f, r, g, out_0, out_1, out_2):
@@ -63,8 +66,8 @@ def tile_factorizedtwoaxisspectraloperator_x1_kernel(tc, x, a, f, r, g, out_0, o
         xh_q, xw_q, vh_q, vw_q = (quantised(n, 2) for n in ("xh", "xw", "vh", "vw"))
         y = tiles("y", 3 * PACK, [P, L], F32)
         y16 = tiles("y16", 2 * PACK, [P, 2, P, 2], BF16)
-        yt = tiles("yt", 2, [P, L, PACK], BF16)
-        y_codes = tiles("y_codes", 2, [P, L], U32)
+        yt = tiles("yt", 3, [P, L, PACK], BF16)
+        y_codes = tiles("y_codes", 3, [P, L], U32)
         y_scales = tiles("y_scales", C // GROUP, [P, L], U8)
 
         def quantise(dst, words):
@@ -161,8 +164,10 @@ def tile_factorizedtwoaxisspectraloperator_x1_kernel(tc, x, a, f, r, g, out_0, o
             )
 
         def modes_w(c, t):
-            bank = sbank(c - 1, 2 + t)
-            mx(bank[:], w_q[F0], block(t), xw_q[c % 2], ALL, True, True)
+            mx(sbank(c, W_USE[t])[:], w_q[F0], block(t), xw_q[c % 2], ALL, True, True)
+
+        def scale_vw(c, t):
+            bank = sbank(c, W_USE[t])
             nc.scalar.activation(out=vw_rows[c % 2][:, t, :], in_=bank[:], func=ACT.Copy, scale=fac32[:, R_ROW + c, t : t + 1])
 
         def interleave_vw(c, cols):
@@ -194,7 +199,7 @@ def tile_factorizedtwoaxisspectraloperator_x1_kernel(tc, x, a, f, r, g, out_0, o
 
         def collect_y(c, js, bank, copy):
             n = P * len(js)
-            words = yt[c % 2][:].rearrange("p n t -> p (n t)").bitcast(F32)
+            words = yt[c % 3][:].rearrange("p n t -> p (n t)").bitcast(F32)
             copy(
                 out=words[:, 2 * P * js[0] : 2 * P * js[0] + 2 * n].rearrange("p (n u) -> p n u", u=2),
                 in_=bank[:, 0 : 2 * n].rearrange("p (u n) -> p n u", u=2),
@@ -204,10 +209,10 @@ def tile_factorizedtwoaxisspectraloperator_x1_kernel(tc, x, a, f, r, g, out_0, o
         scales_out = out_2.rearrange("g q m -> q (g m)").bitcast(I32)
 
         def quantise_y(c, cols):
-            quantise((y_codes[c % 2][:, cols], y_scales[c // GROUP][4 * (c % GROUP) :, cols]), yt[c % 2][:, cols, :])
+            quantise((y_codes[c % 3][:, cols], y_scales[c // GROUP][4 * (c % GROUP) :, cols]), yt[c % 3][:, cols, :])
 
         def store_words(c, cols):
-            codes = y_codes[c % 2]
+            codes = y_codes[c % 3]
             nc.sync.dma_start(out=words_out[:, L * c + cols.start : L * c + cols.stop], in_=codes[:, cols].bitcast(I32))
 
         def planes(c, cols):
@@ -222,25 +227,25 @@ def tile_factorizedtwoaxisspectraloperator_x1_kernel(tc, x, a, f, r, g, out_0, o
                     in_=y_scales[group][32 * quad : 32 * quad + 16, :].bitcast(I32),
                 )
 
-        nc.vector.memset(rows[:], 0.0)
-        nc.scalar.dma_start(out=rows[A_ROW:R_ROW, :], in_=a)
-        nc.scalar.dma_start(out=rows[R_ROW:N_ROWS, :], in_=r.rearrange("q c m -> (q c) m"))
+        nc.gpsimd.memset(rows[:], 0.0)
+        make_identity(nc, ident[:])
         nc.vector.memset(warm[:, 0:1], 0.0)
         nc.scalar.activation(out=warm[:, 8:9], in_=warm[:, 0:1], func=ACT.Gelu_apprx_tanh)
-        make_identity(nc, ident[:])
         load_weight(F1, f[1])
+        nc.sync.dma_start(out=rows[A_ROW:R_ROW, :], in_=a)
+        nc.sync.dma_start(out=rows[R_ROW:N_ROWS, :], in_=r.rearrange("q c m -> (q c) m"))
         load_x_h(0)
-        load_weight(F0, f[0])
         load_x_w(0)
+        load_weight(F0, f[0])
         load_x_w(1)
         load_x_h(1)
         load_weight(G0, g[0])
         load_weight(G1, g[1])
         for c in range(2, C):
-            load_x_h(c)
             load_x_w(c)
+            load_x_h(c)
 
-        bank = scalar_banks[0]
+        bank = scalar_banks[3]
         row_words = rows[:].bitcast(F32)
         for u in range(2):
             nc.tensor.transpose(bank[:, block(u)], row_words[:, u::2], ident[:])
@@ -257,56 +262,70 @@ def tile_factorizedtwoaxisspectraloperator_x1_kernel(tc, x, a, f, r, g, out_0, o
         scale_xw(0, 1)
         transpose_x(1)
         quantise(whole(xh_q[0]), xh[0][:])
-        quantise(whole(w_q[F0]), w_words[F0][:])
         quantise(whole(xw_q[0]), xw[0][:])
+        quantise(whole(w_q[F0]), w_words[F0][:])
         modes_h(0, 0)
         modes_h(0, 1)
-        for t in range(PACK):
-            modes_w(0, t)
         weight_words(G0, nc.scalar.copy)
-        weight_words(G1, nc.scalar.copy)
         scale_xh(1)
 
         HALVES = ((0, 1), (2, 3))
         last = C - 1
         for c in range(last):
-            interleave_xh(c + 1)
+            ahead, behind = c + 1, c - 1
+            interleave_xh(ahead)
             for half in range(2):
-                scale_xw(c + 1, half)
+                scale_xw(ahead, half)
                 modes_h(c, 2 + half)
+                if c >= 1:
+                    result(behind, 1 + half, sbank(c, R_USE + 1 + half))
+            if c >= 1:
+                result(behind, 3, sbank(c, R_USE + 3))
+            else:
+                for t in range(PACK):
+                    modes_w(0, t)
+                    scale_vw(0, t)
+                weight_words(G1, nc.scalar.copy)
             for s in range(PACK):
                 scale_vh(c, s)
             if c + 2 < C:
                 transpose_x(c + 2)
             if c >= 1:
                 for j in range(PACK):
-                    round_y(c - 1, j, nc.scalar.copy)
-                for half in range(2):
-                    transpose_y(c - 1, HALVES[half], sbank(c, half))
-                for half in range(2):
-                    collect_y(c - 1, HALVES[half], sbank(c, half), nc.scalar.copy)
-            quantise(whole(xh_q[(c + 1) % 2]), xh[0][:])
-            quantise(whole(xw_q[(c + 1) % 2]), xw[0][:])
-            for s in range(2 if c + 2 < C else PACK):
-                modes_h(c + 1, s)
-            for t in range(PACK):
-                modes_w(c + 1, t)
+                    round_y(behind, j, nc.scalar.copy)
+            quantise(whole(xh_q[ahead % 2]), xh[0][:])
+            quantise(whole(xw_q[ahead % 2]), xw[0][:])
+            for s in range(2 if ahead < last else PACK):
+                modes_h(ahead, s)
+            for half in range(2):
+                modes_w(ahead, half)
+                if c >= 1:
+                    transpose_y(behind, HALVES[half], sbank(ahead, T_USE[half]))
+            for half in range(2):
+                scale_vw(ahead, half)
+                if c >= 1:
+                    collect_y(behind, HALVES[half], sbank(ahead, T_USE[half]), nc.scalar.copy)
+            for t in range(2, PACK):
+                modes_w(ahead, t)
+                scale_vw(ahead, t)
             interleave_vw(c, ALL)
             quantise(whole(vh_q[c % 2]), vh[0][:])
             quantise_vw(c, ALL)
             if c == 0:
                 quantise(whole(w_q[G0]), w_words[G0][:])
                 quantise(whole(w_q[G1]), w_words[G1][:])
-            for j in range(PACK):
-                result(c, j, sbank(c, 6 + j))
-            if c + 2 < C:
-                if c >= 1:
-                    planes(c - 1, ALL)
-                scale_xh(c + 2)
-            if c == GROUP:
+            result(c, 0, sbank(ahead, R_USE))
+            if c >= 2:
+                planes(c - 2, ALL)
+            if c - 2 == GROUP - 1:
                 store_scales(0, [nc.sync])
+            if c + 2 < C:
+                scale_xh(c + 2)
 
         lower, upper = slice(0, L // 2), slice(L // 2, L)
+        behind = last - 1
+        for j in range(1, PACK):
+            result(behind, j, sbank(last, R_USE + j))
         for s in range(PACK):
             scale_vh(last, s)
         interleave_vw(last, lower)
@@ -315,20 +334,19 @@ def tile_factorizedtwoaxisspectraloperator_x1_kernel(tc, x, a, f, r, g, out_0, o
         interleave_vw(last, upper)
         planes(last - 2, ALL)
         quantise_vw(last, upper)
-        round_y(last - 1, 0, nc.scalar.copy)
-        for j in range(1, PACK):
-            round_y(last - 1, j, nc.vector.tensor_copy)
+        for j in range(PACK):
+            round_y(behind, j, nc.vector.tensor_copy)
         for j in range(PACK):
             result(last, j, vector_banks[j])
         for half in range(2):
-            transpose_y(last - 1, HALVES[half], scalar_banks[half])
+            transpose_y(behind, HALVES[half], scalar_banks[half])
         round_y(last, 0, nc.vector.tensor_copy)
         round_y(last, 1, nc.vector.tensor_copy)
-        collect_y(last - 1, HALVES[0], scalar_banks[0], nc.vector.tensor_copy)
-        collect_y(last - 1, HALVES[1], scalar_banks[1], nc.scalar.copy)
+        collect_y(behind, HALVES[0], scalar_banks[0], nc.vector.tensor_copy)
+        collect_y(behind, HALVES[1], scalar_banks[1], nc.scalar.copy)
         round_y(last, 2, nc.vector.tensor_copy)
         round_y(last, 3, nc.vector.tensor_copy)
-        planes(last - 1, ALL)
+        planes(behind, ALL)
         for j in range(PACK):
             transpose_y(last, (j,), vector_banks[j])
             collect_y(last, (j,), vector_banks[j], nc.scalar.copy)

@@ -51,8 +51,7 @@ def tile_factorizedtwoaxisspectraloperator_x1_kernel(tc, x, a, f, r, g, out_0, o
         fac32 = sb.tile([P, N_ROWS, PACK], F32, name="fac32", align_bytes=64)
         warm = sb.tile([P, 16], F32, name="warm", align_bytes=64)
         a0 = sb.tile([P, PACK], BF16, name="a0", align_bytes=64)
-        x_h = tiles("x_h", C, [P, PACK, L], BF16)
-        x_w = tiles("x_w", C, [P, PACK, L], BF16)
+        x_sb = tiles("x_sb", C, [P, PACK, L], BF16)
         w_raw = tiles("w_raw", 4, [P, PACK, L], BF16)
         w_words = tiles("w_words", 4, [P, L, PACK], BF16)
         w_q = quantised("w", 4)
@@ -102,11 +101,8 @@ def tile_factorizedtwoaxisspectraloperator_x1_kernel(tc, x, a, f, r, g, out_0, o
         def load_weight(i, src):
             nc.sync.dma_start(out=w_raw[i][:], in_=src.rearrange("(p t) n -> p t n", t=PACK))
 
-        def load_x_h(c):
-            nc.sync.dma_start(out=x_h[c][:], in_=x[c].rearrange("(p t) w -> p t w", t=PACK))
-
-        def load_x_w(c):
-            nc.sync.dma_start(out=x_w[c][:], in_=x[c].rearrange("(j p) w -> p j w", p=P))
+        def load_x(c):
+            nc.sync.dma_start(out=x_sb[c][:], in_=x[c].rearrange("(p t) w -> p t w", t=PACK))
 
         def weight_words(i, copy):
             if i in (F0, F1):
@@ -121,7 +117,7 @@ def tile_factorizedtwoaxisspectraloperator_x1_kernel(tc, x, a, f, r, g, out_0, o
         def scale_xh(c):
             for t in range(PACK):
                 nc.vector.tensor_scalar(
-                    out=xh_rows[0][:, t, :], in0=x_h[c][:, t, :], scalar1=fac32[:, A_ROW + 1, t : t + 1], scalar2=None, op0=ALU.mult
+                    out=xh_rows[0][:, t, :], in0=x_sb[c][:, t, :], scalar1=fac32[:, A_ROW + 1, t : t + 1], scalar2=None, op0=ALU.mult
                 )
 
         def interleave_xh(c):
@@ -133,19 +129,19 @@ def tile_factorizedtwoaxisspectraloperator_x1_kernel(tc, x, a, f, r, g, out_0, o
                 nc.gpsimd.tensor_scalar(out=xh[0][:], in0=src, scalar1=1.0, scalar2=0.0, op0=ALU.mult, op1=ALU.add)
 
         def transpose_x(c):
-            words = x_w[c][:].bitcast(F32)
+            words = x_sb[c][:].bitcast(F32)
             for half in range(2):
-                bank = vbank(c - 1, half)
-                for u in range(2):
-                    for j in range(2):
-                        nc.tensor.transpose(bank[:, block(2 * u + j)], words[:, 2 * half + j, u::2], ident[:])
+                bank = vbank(c - 1, half)[:].rearrange("p (j n u) -> p j n u", j=2, u=2)
+                for j in range(2):
+                    for u in range(2):
+                        nc.tensor.transpose(bank[:, j, :, u], words[:, 2 * half + j, u::2], ident[:])
 
         def scale_xw(c, half):
             bank = vbank(c - 1, half)
             nc.vector.tensor_tensor(
-                out=xw[0][:, 256 * half : 256 * (half + 1), :].rearrange("p n (u e) -> p n u e", e=2),
-                in0=bank[:].bitcast(BF16).rearrange("p (u n e) -> p n u e", u=2, e=2),
-                in1=a0[:].rearrange("p (u e) -> p u e", e=2).unsqueeze(1).to_broadcast([P, 256, 2, 2]),
+                out=xw[0][:].rearrange("p (n j) t -> p n j t", j=PACK)[:, :, 2 * half : 2 * half + 2, :],
+                in0=bank[:].bitcast(BF16).rearrange("p (j n t) -> p n j t", j=2, t=PACK),
+                in1=a0[:].unsqueeze(1).unsqueeze(1).to_broadcast([P, P, 2, PACK]),
                 op=ALU.mult,
             )
 
@@ -231,30 +227,26 @@ def tile_factorizedtwoaxisspectraloperator_x1_kernel(tc, x, a, f, r, g, out_0, o
         make_identity(nc, ident[:])
         nc.vector.memset(warm[:, 0:1], 0.0)
         nc.scalar.activation(out=warm[:, 8:9], in_=warm[:, 0:1], func=ACT.Gelu_apprx_tanh)
-        load_weight(F1, f[1])
+        load_x(0)
         nc.sync.dma_start(out=rows[A_ROW:R_ROW, :], in_=a)
         nc.sync.dma_start(out=rows[R_ROW:N_ROWS, :], in_=r.rearrange("q c m -> (q c) m"))
-        load_x_h(0)
-        load_x_w(0)
+        load_weight(F1, f[1])
         load_weight(F0, f[0])
-        load_x_w(1)
-        load_x_h(1)
+        load_x(1)
         load_weight(G0, g[0])
         load_weight(G1, g[1])
         for c in range(2, C):
-            load_x_w(c)
-            load_x_h(c)
+            load_x(c)
 
         bank = scalar_banks[3]
         row_words = rows[:].bitcast(F32)
         for u in range(2):
             nc.tensor.transpose(bank[:, block(u)], row_words[:, u::2], ident[:])
         turned = bank[:, 0 : 2 * P].bitcast(BF16).rearrange("p (u n e) -> p n u e", u=2, e=2)
-        weight_words(F1, nc.vector.tensor_copy)
         nc.vector.tensor_copy(out=fac32[:].rearrange("p n (u e) -> p n u e", e=2), in_=turned[:, 0:N_ROWS])
         nc.vector.tensor_copy(out=a0[:].rearrange("p (u e) -> p u e", e=2), in_=turned[:, A_ROW])
-        quantise(whole(w_q[F1]), w_words[F1][:])
-        weight_words(F0, nc.scalar.copy)
+        for i in (F1, F0, G0, G1):
+            weight_words(i, nc.scalar.copy)
         scale_xh(0)
         transpose_x(0)
         interleave_xh(0)
@@ -263,10 +255,10 @@ def tile_factorizedtwoaxisspectraloperator_x1_kernel(tc, x, a, f, r, g, out_0, o
         transpose_x(1)
         quantise(whole(xh_q[0]), xh[0][:])
         quantise(whole(xw_q[0]), xw[0][:])
+        quantise(whole(w_q[F1]), w_words[F1][:])
         quantise(whole(w_q[F0]), w_words[F0][:])
         modes_h(0, 0)
         modes_h(0, 1)
-        weight_words(G0, nc.scalar.copy)
         scale_xh(1)
 
         HALVES = ((0, 1), (2, 3))
@@ -285,7 +277,6 @@ def tile_factorizedtwoaxisspectraloperator_x1_kernel(tc, x, a, f, r, g, out_0, o
                 for t in range(PACK):
                     modes_w(0, t)
                     scale_vw(0, t)
-                weight_words(G1, nc.scalar.copy)
             for s in range(PACK):
                 scale_vh(c, s)
             if c + 2 < C:
@@ -308,12 +299,12 @@ def tile_factorizedtwoaxisspectraloperator_x1_kernel(tc, x, a, f, r, g, out_0, o
             for t in range(2, PACK):
                 modes_w(ahead, t)
                 scale_vw(ahead, t)
-            interleave_vw(c, ALL)
-            quantise(whole(vh_q[c % 2]), vh[0][:])
-            quantise_vw(c, ALL)
             if c == 0:
                 quantise(whole(w_q[G0]), w_words[G0][:])
                 quantise(whole(w_q[G1]), w_words[G1][:])
+            interleave_vw(c, ALL)
+            quantise(whole(vh_q[c % 2]), vh[0][:])
+            quantise_vw(c, ALL)
             result(c, 0, sbank(ahead, R_USE))
             if c >= 2:
                 planes(c - 2, ALL)

from contextlib import ExitStack

import concourse.mybir as mybir
from concourse.masks import make_identity

C, L, P, PACK = 8, 512, 128, 4
FLOPS = 4 * 2 * C * L * L * L

F32 = mybir.dt.float32
BF16 = mybir.dt.bfloat16
U32 = mybir.dt.uint32
I32 = mybir.dt.int32
U8 = mybir.dt.uint8
FP8X4 = mybir.dt.float8_e4m3fn_x4
ALU = mybir.AluOpType
ACT = mybir.ActivationFunctionType

A_ROW = 0
R_ROW = 2
N_ROWS = 2 + 2 * C
GROUP = 4
W_USE = (0, 2, 4, 5)
T_USE = (1, 3)
R_USE = 6


def tile_factorizedtwoaxisspectraloperator_x1_kernel(tc, x, a, f, r, g, out_0, out_1, out_2):
    nc = tc.nc
    with ExitStack() as ctx:
        sb = ctx.enter_context(tc.tile_pool(name="sb", bufs=1))
        ps = ctx.enter_context(tc.psum_pool(name="ps", bufs=1))
        ctx.enter_context(tc.manual_schedule())

        def tiles(name, count, shape, dtype):
            return [sb.tile(shape, dtype, name="%s%d" % (name, i), align_bytes=64) for i in range(count)]

        def quantised(name, count):
            return list(zip(tiles(name + "_codes", count, [P, L], U32), tiles(name + "_scales", count, [P, L], U8)))

        vector_banks = [ps.tile([P, L], F32, name="vbank%d" % i) for i in range(4)]
        scalar_banks = [ps.tile([P, L], F32, name="sbank%d" % i) for i in range(4)]

        def vbank(c, use):
            return vector_banks[(6 * c + use) % 4]

        def sbank(c, use):
            return scalar_banks[(10 * c + use) % 4]

        ident = sb.tile([P, P], F32, name="ident", align_bytes=64)
        rows = sb.tile([P, L], BF16, name="rows", align_bytes=64)
        fac32 = sb.tile([P, N_ROWS, PACK], F32, name="fac32", align_bytes=64)
        warm = sb.tile([P, 16], F32, name="warm", align_bytes=64)
        a0 = sb.tile([P, PACK], BF16, name="a0", align_bytes=64)
        x_sb = tiles("x_sb", C, [P, PACK, L], BF16)
        w_raw = tiles("w_raw", 4, [P, PACK, L], BF16)
        w_words = tiles("w_words", 4, [P, L, PACK], BF16)
        w_q = quantised("w", 4)
        F0, F1, G0, G1 = range(4)
        xh_rows = tiles("xh_rows", 1, [P, PACK, L], BF16)
        xh = tiles("xh", 1, [P, L, PACK], BF16)
        xw = tiles("xw", 1, [P, L, PACK], BF16)
        vw_rows = tiles("vw_rows", 2, [P, PACK, L], BF16)
        vw = tiles("vw", 1, [P, L, PACK], BF16)
        vh = tiles("vh", 1, [P, L, PACK], BF16)
        xh_q, xw_q, vh_q, vw_q = (quantised(n, 2) for n in ("xh", "xw", "vh", "vw"))
        y = tiles("y", 3 * PACK, [P, L], F32)
        y16 = tiles("y16", 2 * PACK, [P, 2, P, 2], BF16)
        yt = tiles("yt", 3, [P, L, PACK], BF16)
        y_codes = tiles("y_codes", 3, [P, L], U32)
        y_scales = tiles("y_scales", C // GROUP, [P, L], U8)

        def quantise(dst, words):
            codes, scales = dst
            nc.vector.quantize_mx(out=codes.bitcast(FP8X4), scales=scales, in_=words.rearrange("p n t -> p (n t)"))

        def whole(pair):
            return pair[0][:], pair[1][:]

        def mx(out, lhs, lhs_cols, rhs, rhs_cols, start, stop):
            nc.tensor.matmul_mx(
                out=out,
                lhsT=lhs[0][:, lhs_cols].bitcast(FP8X4),
                lhsT_scale=lhs[1][:, lhs_cols],
                rhs=rhs[0][:, rhs_cols].bitcast(FP8X4),
                rhs_scale=rhs[1][:, rhs_cols],
                start=start,
                stop=stop,
            )

        def block(i):
            return slice(P * i, P * (i + 1))

        ALL = slice(0, L)

        def interleave_views(words, slots):
            return (
                words.rearrange("p (c i) t -> p c t i", i=4),
                slots.rearrange("p t (c i) -> p c t i", i=4),
            )

        def load_weight(i, src):
            nc.sync.dma_start(out=w_raw[i][:], in_=src.rearrange("(p t) n -> p t n", t=PACK))

        def load_x(c):
            nc.sync.dma_start(out=x_sb[c][:], in_=x[c].rearrange("(p t) w -> p t w", t=PACK))

        def weight_words(i, copy):
            if i in (F0, F1):
                copy(
                    out=w_words[i][:].rearrange("p (s m) t -> p m t s", s=PACK),
                    in_=w_raw[i][:].rearrange("p t (m s) -> p m t s", s=PACK),
                )
            else:
                dst, src = interleave_views(w_words[i][:], w_raw[i][:])
                copy(out=dst, in_=src)

        def scale_xh(c):
            for t in range(PACK):
                nc.vector.tensor_scalar(
                    out=xh_rows[0][:, t, :], in0=x_sb[c][:, t, :], scalar1=fac32[:, A_ROW + 1, t : t + 1], scalar2=None, op0=ALU.mult
                )

        def interleave_xh(c):
            if c == 0:
                dst, src = interleave_views(xh[0][:], xh_rows[0][:])
                nc.vector.tensor_copy(out=dst, in_=src)
            else:
                src = xh_rows[0][:].rearrange("p t n -> p n t")
                nc.gpsimd.tensor_scalar(out=xh[0][:], in0=src, scalar1=1.0, scalar2=0.0, op0=ALU.mult, op1=ALU.add)

        def transpose_x(c):
            words = x_sb[c][:].bitcast(F32)
            for half in range(2):
                bank = vbank(c - 1, half)[:].rearrange("p (j n u) -> p j n u", j=2, u=2)
                for j in range(2):
                    for u in range(2):
                        nc.tensor.transpose(bank[:, j, :, u], words[:, 2 * half + j, u::2], ident[:])

        def scale_xw(c, half):
            bank = vbank(c - 1, half)
            nc.vector.tensor_tensor(
                out=xw[0][:].rearrange("p (n j) t -> p n j t", j=PACK)[:, :, 2 * half : 2 * half + 2, :],
                in0=bank[:].bitcast(BF16).rearrange("p (j n t) -> p n j t", j=2, t=PACK),
                in1=a0[:].unsqueeze(1).unsqueeze(1).to_broadcast([P, P, 2, PACK]),
                op=ALU.mult,
            )

        def modes_h(c, s):
            bank = vbank(c, 2 + s)
            for t in range(PACK):
                mx(bank[:, block(t)], w_q[F1], block(t), xh_q[c % 2], block(s), True, True)

        def scale_vh(c, s):
            bank = vbank(c, 2 + s)
            nc.vector.tensor_tensor(
                out=vh[0][:, block(s), :],
                in0=bank[:].rearrange("p (t n) -> p n t", t=PACK),
                in1=fac32[:, R_ROW + C + c, :].unsqueeze(1).to_broadcast([P, P, PACK]),
                op=ALU.mult,
            )

        def modes_w(c, t):
            mx(sbank(c, W_USE[t])[:], w_q[F0], block(t), xw_q[c % 2], ALL, True, True)

        def scale_vw(c, t):
            bank = sbank(c, W_USE[t])
            nc.scalar.activation(out=vw_rows[c % 2][:, t, :], in_=bank[:], func=ACT.Copy, scale=fac32[:, R_ROW + c, t : t + 1])

        def interleave_vw(c, cols):
            dst, src = interleave_views(vw[0][:, cols, :], vw_rows[c % 2][:, :, cols])
            nc.vector.tensor_copy(out=dst, in_=src)

        def quantise_vw(c, cols):
            codes, scales = vw_q[c % 2]
            quantise((codes[:, cols], scales[:, cols]), vw[0][:, cols, :])

        def result(c, j, bank):
            mx(bank[:], vw_q[c % 2], block(j), w_q[G0], ALL, True, False)
            mx(bank[:], w_q[G1], block(j), vh_q[c % 2], ALL, False, True)
            tile = y[PACK * (c % 3) + j]
            nc.scalar.activation(out=tile[:], in_=bank[:], func=ACT.Gelu_apprx_tanh)
            nc.sync.dma_start(out=out_0[c, block(j), :], in_=tile[:])

        def round_y(c, j, copy):
            copy(
                out=y16[PACK * (c % 2) + j][:],
                in_=y[PACK * (c % 3) + j][:].rearrange("p (q u e) -> p u q e", u=2, e=2),
            )

        def transpose_y(c, js, bank):
            for u in range(2):
                for i, j in enumerate(js):
                    words = y16[PACK * (c % 2) + j][:].rearrange("p u q e -> p (u q e)").bitcast(F32)
                    nc.tensor.transpose(bank[:, block(len(js) * u + i)], words[:, block(u)], ident[:])

        def collect_y(c, js, bank, copy):
            n = P * len(js)
            words = yt[c % 3][:].rearrange("p n t -> p (n t)").bitcast(F32)
            copy(
                out=words[:, 2 * P * js[0] : 2 * P * js[0] + 2 * n].rearrange("p (n u) -> p n u", u=2),
                in_=bank[:, 0 : 2 * n].rearrange("p (u n) -> p n u", u=2),
            )

        words_out = out_1.rearrange("g p m t -> p (g m t)").bitcast(I32)
        scales_out = out_2.rearrange("g q m -> q (g m)").bitcast(I32)

        def quantise_y(c, cols):
            quantise((y_codes[c % 3][:, cols], y_scales[c // GROUP][4 * (c % GROUP) :, cols]), yt[c % 3][:, cols, :])

        def store_words(c, cols):
            codes = y_codes[c % 3]
            nc.sync.dma_start(out=words_out[:, L * c + cols.start : L * c + cols.stop], in_=codes[:, cols].bitcast(I32))

        def planes(c, cols):
            quantise_y(c, cols)
            store_words(c, cols)

        def store_scales(group, queues):
            first = group * GROUP * (L // 4)
            for quad in range(4):
                queues[quad % len(queues)].dma_start(
                    out=scales_out[4 * quad : 4 * quad + 4, first : first + GROUP * (L // 4)].rearrange("q (k n) -> k q n", k=GROUP),
                    in_=y_scales[group][32 * quad : 32 * quad + 16, :].bitcast(I32),
                )

        nc.gpsimd.memset(rows[:], 0.0)
        make_identity(nc, ident[:])
        nc.vector.memset(warm[:, 0:1], 0.0)
        nc.scalar.activation(out=warm[:, 8:9], in_=warm[:, 0:1], func=ACT.Gelu_apprx_tanh)
        load_x(0)
        nc.sync.dma_start(out=rows[A_ROW:R_ROW, :], in_=a)
        nc.sync.dma_start(out=rows[R_ROW:N_ROWS, :], in_=r.rearrange("q c m -> (q c) m"))
        load_weight(F1, f[1])
        load_weight(F0, f[0])
        load_x(1)
        load_weight(G0, g[0])
        load_weight(G1, g[1])
        for c in range(2, C):
            load_x(c)

        bank = scalar_banks[3]
        row_words = rows[:].bitcast(F32)
        for u in range(2):
            nc.tensor.transpose(bank[:, block(u)], row_words[:, u::2], ident[:])
        turned = bank[:, 0 : 2 * P].bitcast(BF16).rearrange("p (u n e) -> p n u e", u=2, e=2)
        nc.vector.tensor_copy(out=fac32[:].rearrange("p n (u e) -> p n u e", e=2), in_=turned[:, 0:N_ROWS])
        nc.vector.tensor_copy(out=a0[:].rearrange("p (u e) -> p u e", e=2), in_=turned[:, A_ROW])
        for i in (F1, F0, G0, G1):
            weight_words(i, nc.scalar.copy)
        scale_xh(0)
        transpose_x(0)
        interleave_xh(0)
        scale_xw(0, 0)
        scale_xw(0, 1)
        transpose_x(1)
        quantise(whole(xh_q[0]), xh[0][:])
        quantise(whole(xw_q[0]), xw[0][:])
        quantise(whole(w_q[F1]), w_words[F1][:])
        quantise(whole(w_q[F0]), w_words[F0][:])
        modes_h(0, 0)
        modes_h(0, 1)
        scale_xh(1)

        HALVES = ((0, 1), (2, 3))
        last = C - 1
        for c in range(last):
            ahead, behind = c + 1, c - 1
            interleave_xh(ahead)
            for half in range(2):
                scale_xw(ahead, half)
                modes_h(c, 2 + half)
                if c >= 1:
                    result(behind, 1 + half, sbank(c, R_USE + 1 + half))
            if c >= 1:
                result(behind, 3, sbank(c, R_USE + 3))
            else:
                for t in range(PACK):
                    modes_w(0, t)
                    scale_vw(0, t)
            for s in range(PACK):
                scale_vh(c, s)
            if c + 2 < C:
                transpose_x(c + 2)
            if c >= 1:
                for j in range(PACK):
                    round_y(behind, j, nc.scalar.copy)
            quantise(whole(xh_q[ahead % 2]), xh[0][:])
            quantise(whole(xw_q[ahead % 2]), xw[0][:])
            for s in range(2 if ahead < last else PACK):
                modes_h(ahead, s)
            for half in range(2):
                modes_w(ahead, half)
                if c >= 1:
                    transpose_y(behind, HALVES[half], sbank(ahead, T_USE[half]))
            for half in range(2):
                scale_vw(ahead, half)
                if c >= 1:
                    collect_y(behind, HALVES[half], sbank(ahead, T_USE[half]), nc.scalar.copy)
            for t in range(2, PACK):
                modes_w(ahead, t)
                scale_vw(ahead, t)
            if c == 0:
                quantise(whole(w_q[G0]), w_words[G0][:])
                quantise(whole(w_q[G1]), w_words[G1][:])
            interleave_vw(c, ALL)
            quantise(whole(vh_q[c % 2]), vh[0][:])
            quantise_vw(c, ALL)
            result(c, 0, sbank(ahead, R_USE))
            if c >= 2:
                planes(c - 2, ALL)
            if c - 2 == GROUP - 1:
                store_scales(0, [nc.sync])
            if c + 2 < C:
                scale_xh(c + 2)

        lower, upper = slice(0, L // 2), slice(L // 2, L)
        behind = last - 1
        for j in range(1, PACK):
            result(behind, j, sbank(last, R_USE + j))
        for s in range(PACK):
            scale_vh(last, s)
        interleave_vw(last, lower)
        quantise(whole(vh_q[last % 2]), vh[0][:])
        quantise_vw(last, lower)
        interleave_vw(last, upper)
        planes(last - 2, ALL)
        quantise_vw(last, upper)
        for j in range(PACK):
            round_y(behind, j, nc.vector.tensor_copy)
        for j in range(PACK):
            result(last, j, vector_banks[j])
        for half in range(2):
            transpose_y(behind, HALVES[half], scalar_banks[half])
        round_y(last, 0, nc.vector.tensor_copy)
        round_y(last, 1, nc.vector.tensor_copy)
        collect_y(behind, HALVES[0], scalar_banks[0], nc.vector.tensor_copy)
        collect_y(behind, HALVES[1], scalar_banks[1], nc.scalar.copy)
        round_y(last, 2, nc.vector.tensor_copy)
        round_y(last, 3, nc.vector.tensor_copy)
        planes(behind, ALL)
        for j in range(PACK):
            transpose_y(last, (j,), vector_banks[j])
            collect_y(last, (j,), vector_banks[j], nc.scalar.copy)
            quantise_y(last, block(j))
            if j % 2 == 1:
                store_words(last, (lower, upper)[j // 2])
        store_scales(1, [nc.scalar, nc.sync])
